import numpy as np
import ml_dtypes


def mxq(x, axis, fmt="e4m3"):
    dtype, down = {"e4m3": (ml_dtypes.float8_e4m3fn, 7), "e5m2": (ml_dtypes.float8_e5m2, 14)}[fmt]
    v = np.moveaxis(np.asarray(x, np.float32).astype(ml_dtypes.bfloat16).astype(np.float64), axis, -1)
    blocks = v.reshape(v.shape[:-1] + (-1, 32))
    amax = np.abs(blocks).max(-1, keepdims=True)
    byte = np.maximum(np.where(amax > 0, np.frexp(amax)[1] - 1 + 127, 0) - down, 1)
    scale = np.exp2(byte - 127.0)
    codes = (blocks / scale).astype(np.float32).astype(dtype).astype(np.float64)
    return np.moveaxis((codes * scale).reshape(v.shape), -1, axis)


WIDE = False


def mx_kscale(k):
    if not WIDE:
        return np.ones(k)
    levels = np.array([10, -10, 5, -5, 0])
    if k % 512:
        return np.exp2(np.random.permutation(np.resize(levels, k // 32))).repeat(32)
    a = np.empty((k // 512, 16))
    for p in range(k // 512):
        a[p, :8] = np.random.permutation(np.resize(levels, 8))
        for g in range(8):
            far = levels[np.abs(levels - a[p, g]) >= 10]
            a[p, g + 8] = far[np.random.randint(len(far))]
    return np.exp2(a.ravel()).repeat(32)


BF16 = ml_dtypes.bfloat16


def bf(x):
    return np.asarray(x, np.float32).astype(BF16)


def f64(x):
    return np.asarray(x).astype(np.float64)


B, E, Z, R, H = 4096, 1024, 512, 512, 64
G4 = 4 * H
G8 = 8 * H


def sigmoid(v):
    return 1.0 / (1.0 + np.exp(-v))


def draw0():
    s, t, u = mx_kscale(E), mx_kscale(Z), mx_kscale(R)
    return {
        "hh": bf(np.random.standard_normal((B, E)) * s),
        "h": bf(np.random.standard_normal((B, R)) * u),
        "c": bf(np.random.standard_normal((B, H))),
        "wz": bf(np.random.standard_normal((E, Z)) / np.sqrt(E) / s[:, None] * t),
        "bz": bf(0.3 * np.random.standard_normal(Z) * t),
        "wd": bf(np.random.standard_normal((Z, G8)) / np.sqrt(Z) / t[:, None]),
        "wh": bf(np.random.standard_normal((R, G4)) / np.sqrt(R) / u[:, None]),
    }


def generate_scale_and_bias(hh, wz, bz, wd, n_gates):
    z = (mxq(hh, 1, "e4m3") @ mxq(wz, 0, "e4m3")) + bz
    q = mxq(z, 1, "e4m3") @ mxq(wd, 0, "e4m3")
    return q[:, :n_gates], q[:, n_gates:]


def lstm_update(p, c):
    pi, pg, pf, po = np.split(p, 4, axis=-1)
    c1 = sigmoid(pf + 1.0) * c + sigmoid(pi) * np.tanh(pg)
    h1 = sigmoid(po) * np.tanh(c1)
    return h1, c1


def core(hh, h, c, wz, bz, wd, wh):
    d, beta = generate_scale_and_bias(f64(hh), f64(wz), f64(bz), f64(wd), wh.shape[1])
    r = mxq(f64(h), 1, "e4m3") @ mxq(f64(wh), 0, "e4m3")
    p = (1.0 + d) * r + beta
    h1, c1 = lstm_update(p, f64(c))
    return h1, c1


def e4m3fn_bytes(y):
    return np.clip(np.asarray(y, np.float64), -448.0, 448.0).astype(np.float32).astype(ml_dtypes.float8_e4m3fn).view(np.uint8)


def e4m3fn_values(b):
    return np.asarray(b, np.uint8).view(ml_dtypes.float8_e4m3fn).astype(np.float64)


def setup_inputs():
    d = draw0()
    x0 = np.asarray(d['hh']).astype(np.float64)
    s = (np.max(np.abs(x0), axis=(0,), keepdims=True) / 448.0).astype(np.float32)
    out = {}
    for k, v in d.items():
        if k == 'hh':
            out['hh_bytes'] = e4m3fn_bytes(x0 / s.astype(np.float64))
            out['hh_scale'] = s
        else:
            out[k] = v
    return out


def reference(hh_bytes, hh_scale, h, c, wz, bz, wd, wh):
    return core(e4m3fn_values(hh_bytes) * hh_scale.astype(np.float64), h, c, wz, bz, wd, wh)

@@ -1,0 +1,303 @@
+from contextlib import ExitStack
+
+import concourse.mybir as mybir
+from concourse.masks import make_identity
+
+B, E, Z, R, H = 4096, 1024, 512, 512, 64
+G4 = 4 * H
+FLOPS = 2 * B * (E * Z + Z * 2 * G4 + R * G4)
+
+F32 = mybir.dt.float32
+BF16 = mybir.dt.bfloat16
+U32 = mybir.dt.uint32
+U8 = mybir.dt.uint8
+FP8 = mybir.dt.float8_e4m3fn
+FP8X4 = mybir.dt.float8_e4m3fn_x4
+ACT = mybir.ActivationFunctionType
+ALU = mybir.AluOpType
+
+P = 128
+ROWS = B // P
+PAIR = 2
+GROUPS = ROWS // PAIR
+N = PAIR * P
+BANK = 512
+
+
+def tile_hyperlstmgeneratedscalebiasstep_t_kernel(
+    tc, hh_bytes, hh_scale, h, c, wz, bz, wd, wh, out_0, out_1
+):
+    nc = tc.nc
+    hh_v = hh_bytes.rearrange("(p j) k -> p (j k)", j=ROWS)
+    h_v = h.rearrange("(p j) k -> p (j k)", j=ROWS)
+    c_v = c.rearrange("(p j) d -> p (j d)", j=ROWS)
+    h1_v = out_0.rearrange("(p j) d -> p (j d)", j=ROWS)
+    c1_v = out_1.rearrange("(p j) d -> p (j d)", j=ROWS)
+
+    with ExitStack() as ctx:
+        keep = ctx.enter_context(tc.tile_pool(name="keep", bufs=1))
+        inputs = ctx.enter_context(tc.tile_pool(name="inputs", bufs=GROUPS))
+        work = ctx.enter_context(tc.tile_pool(name="work", bufs=3))
+        scaled_pool = ctx.enter_context(tc.tile_pool(name="scaled", bufs=4))
+        outs = ctx.enter_context(tc.tile_pool(name="outs", bufs=4))
+        ring = ctx.enter_context(tc.psum_pool(name="ring", bufs=6))
+        qpool = ctx.enter_context(tc.psum_pool(name="qpool", bufs=1))
+        ctx.enter_context(tc.manual_schedule())
+
+        ident = keep.tile([P, P], F32, name="ident")
+        make_identity(nc, ident[:])
+
+        s_col = keep.tile([P, 2, 4], F32, name="s_col")
+        nc.sync.dma_start(out=s_col[:], in_=hh_scale.rearrange("o (g p t) -> p (o g) t", p=P, t=4))
+        hh_raw, h_raw = {}, {}
+
+        def load_hh(g):
+            t = inputs.tile([P, PAIR * E], U8, name="hh_codes", align_bytes=256)
+            nc.sync.dma_start(out=t[:], in_=hh_v[:, g * PAIR * E : (g + 1) * PAIR * E])
+            hh_raw[g] = t
+
+        def load_h(g):
+            t = inputs.tile([P, PAIR * R], BF16, name="h_rows", align_bytes=256)
+            nc.sync.dma_start(out=t[:], in_=h_v[:, g * PAIR * R : (g + 1) * PAIR * R])
+            h_raw[g] = t
+
+        def load_weight(rows, name):
+            t = keep.tile([P, 4, rows.shape[1]], BF16, name=name, align_bytes=256)
+            nc.sync.dma_start(out=t[:], in_=rows.rearrange("(p j) n -> p j n", j=4))
+            return t
+
+        load_hh(0)
+        wz_raw = [load_weight(wz[0:512, :], "wz_raw0"), load_weight(wz[512:1024, :], "wz_raw1")]
+        load_hh(1)
+        bz_raw = keep.tile([P, 4], BF16, name="bz_raw")
+        nc.sync.dma_start(out=bz_raw[:], in_=bz.rearrange("(p t) -> p t", t=4))
+        wd_raw = load_weight(wd, "wd_raw")
+        wh_raw = load_weight(wh, "wh_raw")
+        load_h(0)
+        load_hh(2)
+        c_sb = keep.tile([P, ROWS * H], BF16, name="c_sb", align_bytes=256)
+        nc.sync.dma_start(out=c_sb[:], in_=c_v)
+        for g in range(1, GROUPS):
+            load_h(g)
+            if g + 2 < GROUPS:
+                load_hh(g + 2)
+
+        s_all = keep.tile([P, E], F32, name="s_all", align_bytes=64)
+        for u in range(2):
+            bank = ring.tile([P, BANK], F32, name="bank")
+            for g in range(2):
+                for e in range(2):
+                    j = 2 * g + e
+                    nc.tensor.transpose(
+                        bank[:, j * P : (j + 1) * P],
+                        s_col[:, g, 2 * u + e : 2 * u + e + 1].to_broadcast([P, P]),
+                        ident[:],
+                    )
+            nc.scalar.copy(
+                out=s_all[:, u * BANK : (u + 1) * BANK].rearrange("m (g p e) -> m g p e", g=2, e=2),
+                in_=bank[:].rearrange("m (g e p) -> m g p e", g=2, e=2),
+            )
+
+        def quantize(pool, src, width, name):
+            codes = pool.tile([P, width // 4], U32, name=name + "_codes", align_bytes=64)
+            scales = pool.tile([P, width // 4], U8, name=name + "_scales", align_bytes=64)
+            nc.vector.quantize_mx(out=codes[:].bitcast(FP8X4), scales=scales[:], in_=src)
+            return codes, scales
+
+        def mx(out, lhs, lcols, rhs, rcols, start, stop):
+            nc.tensor.matmul_mx(
+                out=out,
+                lhsT=lhs[0][:, lcols].bitcast(FP8X4),
+                lhsT_scale=lhs[1][:, lcols],
+                rhs=rhs[0][:, rcols].bitcast(FP8X4),
+                rhs_scale=rhs[1][:, rcols],
+                start=start,
+                stop=stop,
+            )
+
+        def interleave_wz(copy, g):
+            t = keep.tile([P, 4 * Z], BF16, name="wz_il%d" % g, align_bytes=64)
+            copy(
+                out=t[:].rearrange("p (t m j) -> p t m j", t=4, j=4),
+                in_=wz_raw[g][:].rearrange("p j (m t) -> p t m j", t=4),
+            )
+            return t
+
+        def interleave(raw, name):
+            width = raw.shape[2]
+            t = keep.tile([P, 4 * width], BF16, name=name, align_bytes=64)
+            nc.scalar.copy(out=t[:].rearrange("p (n j) -> p n j", j=4), in_=raw[:].rearrange("p j n -> p n j"))
+            return t
+
+        scaled, hh_in, hh_q, z_pairs, x_in, x_q = {}, {}, {}, {}, {}, {}
+        d_bank, beta_bank, r_sb, mod, pre, gates, ig, fc, c1, th = {}, {}, {}, {}, {}, {}, {}, {}, {}, {}
+        weights = {}
+
+        def scale_hh(g, a):
+            t = scaled_pool.tile([P, E], BF16, name="scaled", align_bytes=64)
+            nc.vector.tensor_tensor(
+                out=t[:].rearrange("p (u q e) -> p u q e", u=2, e=2),
+                in0=hh_raw[g][:, a * E : (a + 1) * E].bitcast(FP8).rearrange("p (q u e) -> p u q e", u=2, e=2),
+                in1=s_all[:].rearrange("p (u q e) -> p u q e", u=2, e=2),
+                op=ALU.mult,
+            )
+            scaled[(g, a)] = t
+
+        def turn_hh(g):
+            dst = work.tile([P, PAIR * E], BF16, name="hh_in", align_bytes=64)
+            words = dst[:].bitcast(F32).rearrange("p (g a n u) -> p g a n u", g=2, a=PAIR, u=2)
+            for a in range(PAIR):
+                src = scaled[(g, a)][:].bitcast(F32)
+                bank = ring.tile([P, BANK], F32, name="bank")
+                for j in range(4):
+                    nc.tensor.transpose(bank[:, j * P : (j + 1) * P], src[:, j * P : (j + 1) * P], ident[:])
+                nc.scalar.copy(out=words[:, :, a], in_=bank[:].rearrange("p (u g n) -> p g n u", u=2, g=2))
+            hh_in[g] = dst
+
+        def quantize_hh(g):
+            hh_q[g] = quantize(work, hh_in[g][:], PAIR * E, "hh")
+
+        def embed(g):
+            zp = work.tile([P, 2, N, 2], BF16, name="z_pairs", align_bytes=64)
+            for u in range(2):
+                bank = ring.tile([P, BANK], F32, name="bank")
+                for e in range(2):
+                    t = 2 * u + e
+                    for k in range(2):
+                        mx(bank[:, e * N : (e + 1) * N], weights["wz", k], slice(t * P, (t + 1) * P),
+                           hh_q[g], slice(k * N, (k + 1) * N), k == 0, k == 1)
+                for e in range(2):
+                    t = 2 * u + e
+                    nc.scalar.activation(
+                        out=zp[:, u, :, e], in_=bank[:, e * N : (e + 1) * N], func=ACT.Identity,
+                        bias=weights["bz"][:, t : t + 1],
+                    )
+            z_pairs[g] = zp
+
+        def turn_h(g):
+            dst = work.tile([P, 2 * 4 * N], BF16, name="x_in", align_bytes=64)
+            src = h_raw[g][:].bitcast(F32)
+            bank = ring.tile([P, BANK], F32, name="bank")
+            for a in range(PAIR):
+                for u in range(2):
+                    j = 2 * a + u
+                    nc.tensor.transpose(
+                        bank[:, j * P : (j + 1) * P], src[:, a * 256 + u : (a + 1) * 256 : 2], ident[:]
+                    )
+            nc.scalar.copy(
+                out=dst[:, 0 : 4 * N].bitcast(F32).rearrange("p (a n u) -> p a n u", a=PAIR, u=2),
+                in_=bank[:].rearrange("p (a u n) -> p a n u", a=PAIR, u=2),
+            )
+            x_in[g] = dst
+
+        def interleave_z(g):
+            nc.vector.tensor_copy(
+                out=x_in[g][:, 4 * N : 8 * N].bitcast(F32).rearrange("p (n u) -> p n u", u=2),
+                in_=z_pairs[g][:].rearrange("p u n e -> p (u n e)").bitcast(F32).rearrange("p (u n) -> p n u", u=2),
+            )
+
+        def quantize_x(g):
+            x_q[g] = quantize(work, x_in[g][:], 8 * N, "x")
+
+        def project(g):
+            bank = ring.tile([P, BANK], F32, name="bank")
+            for a in range(PAIR):
+                mx(bank[:, a * G4 : (a + 1) * G4], x_q[g], slice(a * P, (a + 1) * P),
+                   weights["wh"], slice(0, G4), True, True)
+            r = work.tile([P, BANK], F32, name="r_sb")
+            nc.scalar.copy(out=r[:], in_=bank[:])
+            r_sb[g] = r
+            d = qpool.tile([P, BANK], F32, name="d_bank")
+            beta = qpool.tile([P, BANK], F32, name="beta_bank")
+            for a in range(PAIR):
+                cols = slice(N + a * P, N + (a + 1) * P)
+                mx(d[:, a * G4 : (a + 1) * G4], x_q[g], cols, weights["wd"], slice(0, G4), True, True)
+                mx(beta[:, a * G4 : (a + 1) * G4], x_q[g], cols, weights["wd"], slice(G4, 2 * G4), True, True)
+            d_bank[g], beta_bank[g] = d, beta
+
+        def modulate(g):
+            t = work.tile([P, BANK], F32, name="mod")
+            nc.vector.scalar_tensor_tensor(
+                out=t[:], in0=d_bank[g][:], scalar=1.0, in1=r_sb[g][:], op0=ALU.add, op1=ALU.mult
+            )
+            mod[g] = t
+
+        def add_beta(g):
+            t = work.tile([P, BANK], F32, name="pre")
+            nc.vector.tensor_tensor(out=t[:], in0=beta_bank[g][:], in1=mod[g][:], op=ALU.add)
+            pre[g] = t
+
+        def activate(g):
+            t = work.tile([P, PAIR, 4, H], F32, name="gates")
+            src = pre[g][:].rearrange("p (a q d) -> p a q d", a=PAIR, q=4)
+            nc.scalar.activation(out=t[:, :, 0:4:3, :], in_=src[:, :, 0:4:3, :], func=ACT.Sigmoid)
+            nc.scalar.activation(out=t[:, :, 2, :], in_=src[:, :, 2, :], func=ACT.Sigmoid, bias=1.0)
+            nc.scalar.activation(out=t[:, :, 1, :], in_=src[:, :, 1, :], func=ACT.Tanh)
+            gates[g] = t
+
+        def products(g):
+            t = work.tile([P, PAIR, H], F32, name="ig")
+            nc.vector.tensor_tensor(out=t[:], in0=gates[g][:, :, 0, :], in1=gates[g][:, :, 1, :], op=ALU.mult)
+            ig[g] = t
+            f = work.tile([P, PAIR, H], F32, name="fc")
+            c_g = c_sb[:, g * PAIR * H : (g + 1) * PAIR * H].rearrange("p (a d) -> p a d", a=PAIR)
+            nc.vector.tensor_tensor(out=f[:], in0=gates[g][:, :, 2, :], in1=c_g, op=ALU.mult)
+            fc[g] = f
+
+        def new_cell(g):
+            t = outs.tile([P, PAIR, H], F32, name="c1")
+            nc.vector.tensor_tensor(out=t[:], in0=fc[g][:], in1=ig[g][:], op=ALU.add)
+            nc.sync.dma_start(
+                out=c1_v[:, g * PAIR * H : (g + 1) * PAIR * H], in_=t[:].rearrange("p a d -> p (a d)")
+            )
+            c1[g] = t
+
+        def squash(g):
+            t = work.tile([P, PAIR, H], F32, name="th")
+            nc.scalar.activation(out=t[:], in_=c1[g][:], func=ACT.Tanh)
+            th[g] = t
+
+        def new_state(g):
+            t = outs.tile([P, PAIR, H], F32, name="h1")
+            nc.vector.tensor_tensor(out=t[:], in0=gates[g][:, :, 3, :], in1=th[g][:], op=ALU.mult)
+            nc.sync.dma_start(
+                out=h1_v[:, g * PAIR * H : (g + 1) * PAIR * H], in_=t[:].rearrange("p a d -> p (a d)")
+            )
+
+        def at(fn, g, *args):
+            if 0 <= g < GROUPS:
+                fn(g, *args)
+
+        wz_il0 = interleave_wz(nc.scalar.copy, 0)
+        scale_hh(0, 0)
+        scale_hh(0, 1)
+        wz_il1 = interleave_wz(nc.vector.tensor_copy, 1)
+        weights["wz", 0] = quantize(keep, wz_il0[:], 4 * Z, "wz0")
+        bz_f = keep.tile([P, 4], F32, name="bz_f")
+        nc.vector.tensor_copy(out=bz_f[:], in_=bz_raw[:])
+        weights["bz"] = bz_f
+        weights["wz", 1] = quantize(keep, wz_il1[:], 4 * Z, "wz1")
+
+        for s in range(GROUPS + 4):
+            at(quantize_x, s - 2)
+            at(turn_hh, s)
+            if s == 0:
+                wd_il = interleave(wd_raw, "wd_il")
+                wh_il = interleave(wh_raw, "wh_il")
+            at(scale_hh, s + 1, 0)
+            at(products, s - 4)
+            at(embed, s - 1)
+            at(quantize_hh, s)
+            at(new_cell, s - 4)
+            at(scale_hh, s + 1, 1)
+            if s == 1:
+                weights["wd"] = quantize(keep, wd_il[:], 4 * 2 * G4, "wd")
+                weights["wh"] = quantize(keep, wh_il[:], 4 * G4, "wh")
+            at(turn_h, s - 1)
+            at(project, s - 2)
+            at(modulate, s - 2)
+            at(interleave_z, s - 1)
+            at(squash, s - 4)
+            at(activate, s - 3)
+            at(add_beta, s - 2)
+            at(new_state, s - 4)

@@ -17,287 +17,325 @@ ACT = mybir.ActivationFunctionType
 ALU = mybir.AluOpType
 
 P = 128
-ROWS = B // P
-PAIR = 2
-GROUPS = ROWS // PAIR
-N = PAIR * P
+TILES = B // P
 BANK = 512
+SINGLES = 2
+SIZES = [2] * ((TILES - SINGLES) // 2) + [1] * SINGLES
+FIRST = [sum(SIZES[:g]) for g in range(len(SIZES))]
+GROUPS = len(SIZES)
+HH_AT, H_AT, Z_AT, STAGE_COLS = 0, 512, 768, 1024
+AHEAD = 3
+CELL_V = 12
+PINNED = 14
+R_V = 99
+H_V = 99
 
 
 def tile_hyperlstmgeneratedscalebiasstep_t_kernel(
     tc, hh_bytes, hh_scale, h, c, wz, bz, wd, wh, out_0, out_1
 ):
     nc = tc.nc
-    hh_v = hh_bytes.rearrange("(p j) k -> p (j k)", j=ROWS)
-    h_v = h.rearrange("(p j) k -> p (j k)", j=ROWS)
-    c_v = c.rearrange("(p j) d -> p (j d)", j=ROWS)
-    h1_v = out_0.rearrange("(p j) d -> p (j d)", j=ROWS)
-    c1_v = out_1.rearrange("(p j) d -> p (j d)", j=ROWS)
+    hh_v = hh_bytes.rearrange("(p j) k -> p (j k)", j=TILES)
+    h_v = h.rearrange("(p j) k -> p (j k)", j=TILES)
+    c_v = c.rearrange("(p j) d -> p (j d)", j=TILES)
+    h1_v = out_0.rearrange("(p j) d -> p (j d)", j=TILES)
+    c1_v = out_1.rearrange("(p j) d -> p (j d)", j=TILES)
+
+    def cols(g, width):
+        return slice(FIRST[g] * width, (FIRST[g] + SIZES[g]) * width)
 
     with ExitStack() as ctx:
         keep = ctx.enter_context(tc.tile_pool(name="keep", bufs=1))
         inputs = ctx.enter_context(tc.tile_pool(name="inputs", bufs=GROUPS))
         work = ctx.enter_context(tc.tile_pool(name="work", bufs=3))
-        scaled_pool = ctx.enter_context(tc.tile_pool(name="scaled", bufs=4))
-        outs = ctx.enter_context(tc.tile_pool(name="outs", bufs=4))
-        ring = ctx.enter_context(tc.psum_pool(name="ring", bufs=6))
-        qpool = ctx.enter_context(tc.psum_pool(name="qpool", bufs=1))
-        ctx.enter_context(tc.manual_schedule())
+        deep = ctx.enter_context(tc.tile_pool(name="deep", bufs=4))
+        scaled_pool = ctx.enter_context(tc.tile_pool(name="scaled", bufs=6))
+        ring = ctx.enter_context(tc.psum_pool(name="ring", bufs=4))
+        fixed = ctx.enter_context(tc.psum_pool(name="fixed", bufs=1))
 
-        ident = keep.tile([P, P], F32, name="ident")
-        make_identity(nc, ident[:])
+        with tc.manual_schedule():
+            ident = keep.tile([P, P], F32, name="ident")
+            make_identity(nc, ident[:])
 
-        s_col = keep.tile([P, 2, 4], F32, name="s_col")
-        nc.sync.dma_start(out=s_col[:], in_=hh_scale.rearrange("o (g p t) -> p (o g) t", p=P, t=4))
-        hh_raw, h_raw = {}, {}
+            s_col = keep.tile([P, 2, 4], F32, name="s_col")
+            nc.sync.dma_start(out=s_col[:], in_=hh_scale.rearrange("o (g p t) -> p (o g) t", p=P, t=4))
+            hh_raw, h_raw = {}, {}
 
-        def load_hh(g):
-            t = inputs.tile([P, PAIR * E], U8, name="hh_codes", align_bytes=256)
-            nc.sync.dma_start(out=t[:], in_=hh_v[:, g * PAIR * E : (g + 1) * PAIR * E])
-            hh_raw[g] = t
+            def load_hh(g):
+                t = inputs.tile([P, SIZES[g] * E], U8, name="hh_codes", align_bytes=256)
+                nc.sync.dma_start(out=t[:], in_=hh_v[:, cols(g, E)])
+                hh_raw[g] = t
 
-        def load_h(g):
-            t = inputs.tile([P, PAIR * R], BF16, name="h_rows", align_bytes=256)
-            nc.sync.dma_start(out=t[:], in_=h_v[:, g * PAIR * R : (g + 1) * PAIR * R])
-            h_raw[g] = t
+            def load_h(g):
+                t = inputs.tile([P, SIZES[g] * R], BF16, name="h_rows", align_bytes=256)
+                nc.sync.dma_start(out=t[:], in_=h_v[:, cols(g, R)])
+                h_raw[g] = t
 
-        def load_weight(rows, name):
-            t = keep.tile([P, 4, rows.shape[1]], BF16, name=name, align_bytes=256)
-            nc.sync.dma_start(out=t[:], in_=rows.rearrange("(p j) n -> p j n", j=4))
-            return t
+            def load_weight(rows, name):
+                t = keep.tile([P, 4, rows.shape[1]], BF16, name=name, align_bytes=256)
+                nc.sync.dma_start(out=t[:], in_=rows.rearrange("(p j) n -> p j n", j=4))
+                return t
 
-        load_hh(0)
-        wz_raw = [load_weight(wz[0:512, :], "wz_raw0"), load_weight(wz[512:1024, :], "wz_raw1")]
-        load_hh(1)
-        bz_raw = keep.tile([P, 4], BF16, name="bz_raw")
-        nc.sync.dma_start(out=bz_raw[:], in_=bz.rearrange("(p t) -> p t", t=4))
-        wd_raw = load_weight(wd, "wd_raw")
-        wh_raw = load_weight(wh, "wh_raw")
-        load_h(0)
-        load_hh(2)
-        c_sb = keep.tile([P, ROWS * H], BF16, name="c_sb", align_bytes=256)
-        nc.sync.dma_start(out=c_sb[:], in_=c_v)
-        for g in range(1, GROUPS):
-            load_h(g)
-            if g + 2 < GROUPS:
-                load_hh(g + 2)
+            load_hh(0)
+            wz_raw = [load_weight(wz[0:512, :], "wz_raw0"), load_weight(wz[512:1024, :], "wz_raw1")]
+            load_hh(1)
+            bz_raw = keep.tile([P, 4], BF16, name="bz_raw")
+            nc.sync.dma_start(out=bz_raw[:], in_=bz.rearrange("(p t) -> p t", t=4))
+            wh_raw = load_weight(wh, "wh_raw")
+            load_h(0)
+            wd_raw = load_weight(wd, "wd_raw")
+            load_hh(2)
+            c_sb = keep.tile([P, TILES * H], BF16, name="c_sb", align_bytes=256)
+            for g in range(1, GROUPS):
+                load_h(g)
+                if g + 2 < GROUPS:
+                    load_hh(g + 2)
+                if g == 1:
+                    nc.sync.dma_start(out=c_sb[:], in_=c_v)
 
-        s_all = keep.tile([P, E], F32, name="s_all", align_bytes=64)
-        for u in range(2):
-            bank = ring.tile([P, BANK], F32, name="bank")
-            for g in range(2):
-                for e in range(2):
-                    j = 2 * g + e
-                    nc.tensor.transpose(
-                        bank[:, j * P : (j + 1) * P],
-                        s_col[:, g, 2 * u + e : 2 * u + e + 1].to_broadcast([P, P]),
-                        ident[:],
-                    )
-            nc.scalar.copy(
-                out=s_all[:, u * BANK : (u + 1) * BANK].rearrange("m (g p e) -> m g p e", g=2, e=2),
-                in_=bank[:].rearrange("m (g e p) -> m g p e", g=2, e=2),
-            )
+            s_bank = []
+            for k in range(2):
+                bank = fixed.tile([P, BANK], F32, name="s_bank%d" % k)
+                for t in range(4):
+                    nc.tensor.transpose(bank[:, t:BANK:4], s_col[:, k, t : t + 1].to_broadcast([P, P]), ident[:])
+                s_bank.append(bank)
 
-        def quantize(pool, src, width, name):
-            codes = pool.tile([P, width // 4], U32, name=name + "_codes", align_bytes=64)
-            scales = pool.tile([P, width // 4], U8, name=name + "_scales", align_bytes=64)
-            nc.vector.quantize_mx(out=codes[:].bitcast(FP8X4), scales=scales[:], in_=src)
+        def quantize_weight(src, name):
+            width = src.shape[1] // 4
+            codes = keep.tile([P, width], U32, name=name + "_codes", align_bytes=64)
+            scales = keep.tile([P, width], U8, name=name + "_scales", align_bytes=64)
+            nc.vector.quantize_mx(out=codes[:].bitcast(FP8X4), scales=scales[:], in_=src[:])
             return codes, scales
 
-        def mx(out, lhs, lcols, rhs, rcols, start, stop):
+        def mx(out, lhs, l0, rhs, r0, start=True, stop=True):
+            n = out.shape[1]
             nc.tensor.matmul_mx(
                 out=out,
-                lhsT=lhs[0][:, lcols].bitcast(FP8X4),
-                lhsT_scale=lhs[1][:, lcols],
-                rhs=rhs[0][:, rcols].bitcast(FP8X4),
-                rhs_scale=rhs[1][:, rcols],
+                lhsT=lhs[0][:, l0 : l0 + P].bitcast(FP8X4),
+                lhsT_scale=lhs[1][:, l0 : l0 + P],
+                rhs=rhs[0][:, r0 : r0 + n].bitcast(FP8X4),
+                rhs_scale=rhs[1][:, r0 : r0 + n],
                 start=start,
                 stop=stop,
             )
 
-        def interleave_wz(copy, g):
-            t = keep.tile([P, 4 * Z], BF16, name="wz_il%d" % g, align_bytes=64)
+        def interleave_wz(copy, k):
+            t = keep.tile([P, 4 * Z], BF16, name="wz_il%d" % k, align_bytes=64)
             copy(
                 out=t[:].rearrange("p (t m j) -> p t m j", t=4, j=4),
-                in_=wz_raw[g][:].rearrange("p j (m t) -> p t m j", t=4),
+                in_=wz_raw[k][:].rearrange("p j (m t) -> p t m j", t=4),
             )
             return t
 
-        def interleave(raw, name):
-            width = raw.shape[2]
-            t = keep.tile([P, 4 * width], BF16, name=name, align_bytes=64)
-            nc.scalar.copy(out=t[:].rearrange("p (n j) -> p n j", j=4), in_=raw[:].rearrange("p j n -> p n j"))
+        def interleave(copy, raw, name):
+            t = keep.tile([P, 4 * raw.shape[2]], BF16, name=name, align_bytes=64)
+            copy(out=t[:].rearrange("p (n j) -> p n j", j=4), in_=raw[:].rearrange("p j n -> p n j"))
             return t
 
-        scaled, hh_in, hh_q, z_pairs, x_in, x_q = {}, {}, {}, {}, {}, {}
+        scaled, staged, act_q, z_pairs = {}, {}, {}, {}
         d_bank, beta_bank, r_sb, mod, pre, gates, ig, fc, c1, th = {}, {}, {}, {}, {}, {}, {}, {}, {}, {}
         weights = {}
+        halves = [(g, a, k) for g in range(GROUPS) for a in range(SIZES[g]) for k in range(2)]
 
-        def scale_hh(g, a):
-            t = scaled_pool.tile([P, E], BF16, name="scaled", align_bytes=64)
+        def cell_engine(g):
+            return nc.vector if g >= CELL_V else nc.gpsimd
+
+        def scale_hh(j):
+            if j >= len(halves):
+                return
+            g, a, k = halves[j]
+            if k == 0:
+                scaled[(g, a)] = scaled_pool.tile([P, E], BF16, name="scaled", align_bytes=64)
             nc.vector.tensor_tensor(
-                out=t[:].rearrange("p (u q e) -> p u q e", u=2, e=2),
-                in0=hh_raw[g][:, a * E : (a + 1) * E].bitcast(FP8).rearrange("p (q u e) -> p u q e", u=2, e=2),
-                in1=s_all[:].rearrange("p (u q e) -> p u q e", u=2, e=2),
+                out=scaled[(g, a)][:, k * BANK : (k + 1) * BANK],
+                in0=hh_raw[g][:, a * E + k * BANK : a * E + (k + 1) * BANK].bitcast(FP8),
+                in1=s_bank[k][:],
                 op=ALU.mult,
             )
-            scaled[(g, a)] = t
+
+        def staging(s, at_col, width):
+            if s not in staged:
+                staged[s] = work.tile([P, 4 * STAGE_COLS], BF16, name="staged", align_bytes=64)
+            return staged[s][:, 4 * at_col : 4 * (at_col + width)]
 
         def turn_hh(g):
-            dst = work.tile([P, PAIR * E], BF16, name="hh_in", align_bytes=64)
-            words = dst[:].bitcast(F32).rearrange("p (g a n u) -> p g a n u", g=2, a=PAIR, u=2)
-            for a in range(PAIR):
+            nt = SIZES[g]
+            words = staging(g, HH_AT, 2 * nt * P).bitcast(F32).rearrange("p (k a n u) -> p k a n u", k=2, a=nt, u=2)
+            for a in range(nt):
                 src = scaled[(g, a)][:].bitcast(F32)
                 bank = ring.tile([P, BANK], F32, name="bank")
-                for j in range(4):
-                    nc.tensor.transpose(bank[:, j * P : (j + 1) * P], src[:, j * P : (j + 1) * P], ident[:])
-                nc.scalar.copy(out=words[:, :, a], in_=bank[:].rearrange("p (u g n) -> p g n u", u=2, g=2))
-            hh_in[g] = dst
+                for k in range(2):
+                    for u in range(2):
+                        j = 2 * k + u
+                        nc.tensor.transpose(
+                            bank[:, j * P : (j + 1) * P], src[:, k * 256 + u : (k + 1) * 256 : 2], ident[:]
+                        )
+                nc.scalar.copy(out=words[:, :, a], in_=bank[:].rearrange("p (k u n) -> p k n u", u=2, k=2))
 
-        def quantize_hh(g):
-            hh_q[g] = quantize(work, hh_in[g][:], PAIR * E, "hh")
+        def quantize_step(s):
+            parts = [(at_col, per_tile * SIZES[g])
+                     for at_col, per_tile, g in ((Z_AT, P, s - 2), (HH_AT, 2 * P, s), (H_AT, P, s - 1))
+                     if 0 <= g < GROUPS]
+            if sum(w for at_col, w in parts) == STAGE_COLS:
+                parts = [(0, STAGE_COLS)]
+            codes = work.tile([P, STAGE_COLS], U32, name="act_codes", align_bytes=64)
+            scales = work.tile([P, STAGE_COLS], U8, name="act_scales", align_bytes=64)
+            for at_col, w in parts:
+                nc.vector.quantize_mx(
+                    out=codes[:, at_col : at_col + w].bitcast(FP8X4),
+                    scales=scales[:, at_col : at_col + w],
+                    in_=staging(s, at_col, w),
+                )
+            act_q[s] = (codes, scales)
 
         def embed(g):
-            zp = work.tile([P, 2, N, 2], BF16, name="z_pairs", align_bytes=64)
+            n = SIZES[g] * P
+            zp = work.tile([P, 2, n, 2], BF16, name="z_pairs", align_bytes=64)
             for u in range(2):
                 bank = ring.tile([P, BANK], F32, name="bank")
                 for e in range(2):
-                    t = 2 * u + e
                     for k in range(2):
-                        mx(bank[:, e * N : (e + 1) * N], weights["wz", k], slice(t * P, (t + 1) * P),
-                           hh_q[g], slice(k * N, (k + 1) * N), k == 0, k == 1)
+                        mx(bank[:, e * n : (e + 1) * n], weights["wz", k], (2 * u + e) * P,
+                           act_q[g], HH_AT + k * n, k == 0, k == 1)
                 for e in range(2):
                     t = 2 * u + e
                     nc.scalar.activation(
-                        out=zp[:, u, :, e], in_=bank[:, e * N : (e + 1) * N], func=ACT.Identity,
+                        out=zp[:, u, :, e], in_=bank[:, e * n : (e + 1) * n], func=ACT.Identity,
                         bias=weights["bz"][:, t : t + 1],
                     )
             z_pairs[g] = zp
 
         def turn_h(g):
-            dst = work.tile([P, 2 * 4 * N], BF16, name="x_in", align_bytes=64)
+            nt = SIZES[g]
             src = h_raw[g][:].bitcast(F32)
             bank = ring.tile([P, BANK], F32, name="bank")
-            for a in range(PAIR):
+            for a in range(nt):
                 for u in range(2):
                     j = 2 * a + u
                     nc.tensor.transpose(
                         bank[:, j * P : (j + 1) * P], src[:, a * 256 + u : (a + 1) * 256 : 2], ident[:]
                     )
-            nc.scalar.copy(
-                out=dst[:, 0 : 4 * N].bitcast(F32).rearrange("p (a n u) -> p a n u", a=PAIR, u=2),
-                in_=bank[:].rearrange("p (a u n) -> p a n u", a=PAIR, u=2),
+            (nc.vector.tensor_copy if g >= H_V else nc.scalar.copy)(
+                out=staging(g + 1, H_AT, nt * P).bitcast(F32).rearrange("p (a n u) -> p a n u", a=nt, u=2),
+                in_=bank[:, 0 : 2 * nt * P].rearrange("p (a u n) -> p a n u", a=nt, u=2),
             )
-            x_in[g] = dst
 
         def interleave_z(g):
             nc.vector.tensor_copy(
-                out=x_in[g][:, 4 * N : 8 * N].bitcast(F32).rearrange("p (n u) -> p n u", u=2),
+                out=staging(g + 2, Z_AT, SIZES[g] * P).bitcast(F32).rearrange("p (n u) -> p n u", u=2),
                 in_=z_pairs[g][:].rearrange("p u n e -> p (u n e)").bitcast(F32).rearrange("p (u n) -> p n u", u=2),
             )
 
-        def quantize_x(g):
-            x_q[g] = quantize(work, x_in[g][:], 8 * N, "x")
-
-        def project(g):
+        def recur(g):
+            nt = SIZES[g]
             bank = ring.tile([P, BANK], F32, name="bank")
-            for a in range(PAIR):
-                mx(bank[:, a * G4 : (a + 1) * G4], x_q[g], slice(a * P, (a + 1) * P),
-                   weights["wh"], slice(0, G4), True, True)
-            r = work.tile([P, BANK], F32, name="r_sb")
-            nc.scalar.copy(out=r[:], in_=bank[:])
+            for a in range(nt):
+                mx(bank[:, a * G4 : (a + 1) * G4], act_q[g + 1], H_AT + a * P, weights["wh"], 0)
+            r = deep.tile([P, nt * G4], F32, name="r_sb")
+            (nc.vector.tensor_copy if g >= R_V else nc.scalar.copy)(out=r[:], in_=bank[:, 0 : nt * G4])
             r_sb[g] = r
-            d = qpool.tile([P, BANK], F32, name="d_bank")
-            beta = qpool.tile([P, BANK], F32, name="beta_bank")
-            for a in range(PAIR):
-                cols = slice(N + a * P, N + (a + 1) * P)
-                mx(d[:, a * G4 : (a + 1) * G4], x_q[g], cols, weights["wd"], slice(0, G4), True, True)
-                mx(beta[:, a * G4 : (a + 1) * G4], x_q[g], cols, weights["wd"], slice(G4, 2 * G4), True, True)
+
+        def generate(g):
+            d = fixed.tile([P, BANK], F32, name="d_bank")
+            beta = fixed.tile([P, BANK], F32, name="beta_bank")
+            for a in range(SIZES[g]):
+                mx(d[:, a * G4 : (a + 1) * G4], act_q[g + 2], Z_AT + a * P, weights["wd"], 0)
+                mx(beta[:, a * G4 : (a + 1) * G4], act_q[g + 2], Z_AT + a * P, weights["wd"], G4)
             d_bank[g], beta_bank[g] = d, beta
 
         def modulate(g):
-            t = work.tile([P, BANK], F32, name="mod")
+            w = SIZES[g] * G4
+            t = work.tile([P, w], F32, name="mod")
             nc.vector.scalar_tensor_tensor(
-                out=t[:], in0=d_bank[g][:], scalar=1.0, in1=r_sb[g][:], op0=ALU.add, op1=ALU.mult
+                out=t[:], in0=d_bank[g][:, 0:w], scalar=1.0, in1=r_sb[g][:], op0=ALU.add, op1=ALU.mult
             )
             mod[g] = t
 
         def add_beta(g):
-            t = work.tile([P, BANK], F32, name="pre")
-            nc.vector.tensor_tensor(out=t[:], in0=beta_bank[g][:], in1=mod[g][:], op=ALU.add)
+            w = SIZES[g] * G4
+            t = work.tile([P, w], F32, name="pre")
+            nc.vector.tensor_tensor(out=t[:], in0=beta_bank[g][:, 0:w], in1=mod[g][:], op=ALU.add)
             pre[g] = t
 
         def activate(g):
-            t = work.tile([P, PAIR, 4, H], F32, name="gates")
-            src = pre[g][:].rearrange("p (a q d) -> p a q d", a=PAIR, q=4)
-            nc.scalar.activation(out=t[:, :, 0:4:3, :], in_=src[:, :, 0:4:3, :], func=ACT.Sigmoid)
+            t = work.tile([P, SIZES[g], 4, H], F32, name="gates")
+            src = pre[g][:].rearrange("p (a q d) -> p a q d", q=4, d=H)
             nc.scalar.activation(out=t[:, :, 2, :], in_=src[:, :, 2, :], func=ACT.Sigmoid, bias=1.0)
             nc.scalar.activation(out=t[:, :, 1, :], in_=src[:, :, 1, :], func=ACT.Tanh)
+            nc.scalar.activation(out=t[:, :, 0:4:3, :], in_=src[:, :, 0:4:3, :], func=ACT.Sigmoid)
             gates[g] = t
 
         def products(g):
-            t = work.tile([P, PAIR, H], F32, name="ig")
-            nc.vector.tensor_tensor(out=t[:], in0=gates[g][:, :, 0, :], in1=gates[g][:, :, 1, :], op=ALU.mult)
-            ig[g] = t
-            f = work.tile([P, PAIR, H], F32, name="fc")
-            c_g = c_sb[:, g * PAIR * H : (g + 1) * PAIR * H].rearrange("p (a d) -> p a d", a=PAIR)
-            nc.vector.tensor_tensor(out=f[:], in0=gates[g][:, :, 2, :], in1=c_g, op=ALU.mult)
+            f = work.tile([P, SIZES[g], H], F32, name="fc")
+            c_g = c_sb[:, cols(g, H)].rearrange("p (a d) -> p a d", d=H)
+            cell_engine(g).tensor_tensor(out=f[:], in0=gates[g][:, :, 2, :], in1=c_g, op=ALU.mult)
             fc[g] = f
+            t = work.tile([P, SIZES[g], H], F32, name="ig")
+            cell_engine(g).tensor_tensor(out=t[:], in0=gates[g][:, :, 0, :], in1=gates[g][:, :, 1, :], op=ALU.mult)
+            ig[g] = t
 
         def new_cell(g):
-            t = outs.tile([P, PAIR, H], F32, name="c1")
-            nc.vector.tensor_tensor(out=t[:], in0=fc[g][:], in1=ig[g][:], op=ALU.add)
-            nc.sync.dma_start(
-                out=c1_v[:, g * PAIR * H : (g + 1) * PAIR * H], in_=t[:].rearrange("p a d -> p (a d)")
-            )
+            t = deep.tile([P, SIZES[g], H], F32, name="c1")
+            cell_engine(g).tensor_tensor(out=t[:], in0=fc[g][:], in1=ig[g][:], op=ALU.add)
+            nc.sync.dma_start(out=c1_v[:, cols(g, H)], in_=t[:].rearrange("p a d -> p (a d)"))
             c1[g] = t
 
         def squash(g):
-            t = work.tile([P, PAIR, H], F32, name="th")
+            t = work.tile([P, SIZES[g], H], F32, name="th")
             nc.scalar.activation(out=t[:], in_=c1[g][:], func=ACT.Tanh)
             th[g] = t
 
         def new_state(g):
-            t = outs.tile([P, PAIR, H], F32, name="h1")
-            nc.vector.tensor_tensor(out=t[:], in0=gates[g][:, :, 3, :], in1=th[g][:], op=ALU.mult)
-            nc.sync.dma_start(
-                out=h1_v[:, g * PAIR * H : (g + 1) * PAIR * H], in_=t[:].rearrange("p a d -> p (a d)")
-            )
+            t = deep.tile([P, SIZES[g], H], F32, name="h1")
+            cell_engine(g).tensor_tensor(out=t[:], in0=gates[g][:, :, 3, :], in1=th[g][:], op=ALU.mult)
+            nc.sync.dma_start(out=h1_v[:, cols(g, H)], in_=t[:].rearrange("p a d -> p (a d)"))
 
-        def at(fn, g, *args):
+        def at(fn, g):
             if 0 <= g < GROUPS:
-                fn(g, *args)
+                fn(g)
 
-        wz_il0 = interleave_wz(nc.scalar.copy, 0)
-        scale_hh(0, 0)
-        scale_hh(0, 1)
-        wz_il1 = interleave_wz(nc.vector.tensor_copy, 1)
-        weights["wz", 0] = quantize(keep, wz_il0[:], 4 * Z, "wz0")
-        bz_f = keep.tile([P, 4], F32, name="bz_f")
-        nc.vector.tensor_copy(out=bz_f[:], in_=bz_raw[:])
-        weights["bz"] = bz_f
-        weights["wz", 1] = quantize(keep, wz_il1[:], 4 * Z, "wz1")
-
-        for s in range(GROUPS + 4):
-            at(quantize_x, s - 2)
+        def step(s):
+            j = 2 * AHEAD + 4 * s
             at(turn_hh, s)
             if s == 0:
-                wd_il = interleave(wd_raw, "wd_il")
-                wh_il = interleave(wh_raw, "wh_il")
-            at(scale_hh, s + 1, 0)
-            at(products, s - 4)
-            at(embed, s - 1)
-            at(quantize_hh, s)
-            at(new_cell, s - 4)
-            at(scale_hh, s + 1, 1)
+                weights["wh_il"] = interleave(nc.scalar.copy, wh_raw, "wh_il")
+                weights["wd_il"] = interleave(nc.scalar.copy, wd_raw, "wd_il")
+            scale_hh(j)
+            at(add_beta, s - 3)
+            if s < GROUPS + 2:
+                quantize_step(s)
             if s == 1:
-                weights["wd"] = quantize(keep, wd_il[:], 4 * 2 * G4, "wd")
-                weights["wh"] = quantize(keep, wh_il[:], 4 * G4, "wh")
-            at(turn_h, s - 1)
-            at(project, s - 2)
-            at(modulate, s - 2)
+                weights["wh"] = quantize_weight(weights["wh_il"], "wh")
+                weights["wd"] = quantize_weight(weights["wd_il"], "wd")
+            at(embed, s - 1)
             at(interleave_z, s - 1)
             at(squash, s - 4)
             at(activate, s - 3)
-            at(add_beta, s - 2)
             at(new_state, s - 4)
+            at(products, s - 3)
+            at(new_cell, s - 3)
+            scale_hh(j + 1)
+            scale_hh(j + 2)
+            scale_hh(j + 3)
+            at(turn_h, s)
+            at(generate, s - 2)
+            at(recur, s - 1)
+            at(modulate, s - 2)
+
+        with tc.manual_schedule():
+            wz_il0 = interleave_wz(nc.scalar.copy, 0)
+            for j in range(4):
+                scale_hh(j)
+            wz_il1 = interleave_wz(nc.vector.tensor_copy, 1)
+            weights["wz", 0] = quantize_weight(wz_il0, "wz0")
+            bz_f = keep.tile([P, 4], F32, name="bz_f")
+            nc.vector.tensor_copy(out=bz_f[:], in_=bz_raw[:])
+            weights["bz"] = bz_f
+            weights["wz", 1] = quantize_weight(wz_il1, "wz1")
+            for j in range(4, 2 * AHEAD):
+                scale_hh(j)
+
+            for s in range(PINNED):
+                step(s)
+        for s in range(PINNED, GROUPS + 4):
+            step(s)

@@ -17,32 +17,33 @@ ACT = mybir.ActivationFunctionType
 ALU = mybir.AluOpType
 
 P = 128
-TILES = B // P
+PACK = 4
+K_PASS = P * PACK
+PAIRS = K_PASS // 2
 BANK = 512
-SINGLES = 2
-SIZES = [2] * ((TILES - SINGLES) // 2) + [1] * SINGLES
-FIRST = [sum(SIZES[:g]) for g in range(len(SIZES))]
-GROUPS = len(SIZES)
-HH_AT, H_AT, Z_AT, STAGE_COLS = 0, 512, 768, 1024
-AHEAD = 3
-CELL_V = 12
-PINNED = 14
-R_V = 99
-H_V = 99
+TILES = B // P
+PAIR = 2
+N = PAIR * P
+GROUPS = TILES // PAIR
+
+HH_AT, H_AT, Z_AT, STEP_COLS = 0, 2 * N, 3 * N, 4 * N
+
+SCALING_STEPS = GROUPS - 1
+LAST_LAG = 5
 
 
 def tile_hyperlstmgeneratedscalebiasstep_t_kernel(
     tc, hh_bytes, hh_scale, h, c, wz, bz, wd, wh, out_0, out_1
 ):
     nc = tc.nc
-    hh_v = hh_bytes.rearrange("(p j) k -> p (j k)", j=TILES)
-    h_v = h.rearrange("(p j) k -> p (j k)", j=TILES)
-    c_v = c.rearrange("(p j) d -> p (j d)", j=TILES)
-    h1_v = out_0.rearrange("(p j) d -> p (j d)", j=TILES)
-    c1_v = out_1.rearrange("(p j) d -> p (j d)", j=TILES)
+    hh_rows = hh_bytes.rearrange("(p j) k -> p (j k)", j=TILES)
+    h_rows = h.rearrange("(p j) k -> p (j k)", j=TILES)
+    c_rows = c.rearrange("(p j) d -> p (j d)", j=TILES)
+    h1_rows = out_0.rearrange("(p j) d -> p (j d)", j=TILES)
+    c1_rows = out_1.rearrange("(p j) d -> p (j d)", j=TILES)
 
     def cols(g, width):
-        return slice(FIRST[g] * width, (FIRST[g] + SIZES[g]) * width)
+        return slice(g * PAIR * width, (g + 1) * PAIR * width)
 
     with ExitStack() as ctx:
         keep = ctx.enter_context(tc.tile_pool(name="keep", bufs=1))
@@ -53,289 +54,277 @@ def tile_hyperlstmgeneratedscalebiasstep_t_kernel(
         ring = ctx.enter_context(tc.psum_pool(name="ring", bufs=4))
         fixed = ctx.enter_context(tc.psum_pool(name="fixed", bufs=1))
 
+        hh_raw, h_raw = {}, {}
+
+        def load_hh(g):
+            t = inputs.tile([P, PAIR * E], U8, name="hh_codes", align_bytes=256)
+            nc.sync.dma_start(out=t[:], in_=hh_rows[:, cols(g, E)])
+            hh_raw[g] = t
+
+        def load_h(g):
+            t = inputs.tile([P, PAIR * R], BF16, name="h_values", align_bytes=256)
+            nc.sync.dma_start(out=t[:], in_=h_rows[:, cols(g, R)])
+            h_raw[g] = t
+
+        def load_weight(rows, name):
+            t = keep.tile([P, PACK, rows.shape[1]], BF16, name=name, align_bytes=256)
+            nc.sync.dma_start(out=t[:], in_=rows.rearrange("(p t) n -> p t n", t=PACK))
+            return t
+
         with tc.manual_schedule():
             ident = keep.tile([P, P], F32, name="ident")
             make_identity(nc, ident[:])
 
-            s_col = keep.tile([P, 2, 4], F32, name="s_col")
-            nc.sync.dma_start(out=s_col[:], in_=hh_scale.rearrange("o (g p t) -> p (o g) t", p=P, t=4))
-            hh_raw, h_raw = {}, {}
-
-            def load_hh(g):
-                t = inputs.tile([P, SIZES[g] * E], U8, name="hh_codes", align_bytes=256)
-                nc.sync.dma_start(out=t[:], in_=hh_v[:, cols(g, E)])
-                hh_raw[g] = t
-
-            def load_h(g):
-                t = inputs.tile([P, SIZES[g] * R], BF16, name="h_rows", align_bytes=256)
-                nc.sync.dma_start(out=t[:], in_=h_v[:, cols(g, R)])
-                h_raw[g] = t
-
-            def load_weight(rows, name):
-                t = keep.tile([P, 4, rows.shape[1]], BF16, name=name, align_bytes=256)
-                nc.sync.dma_start(out=t[:], in_=rows.rearrange("(p j) n -> p j n", j=4))
-                return t
-
+            s_col = keep.tile([P, 2, PACK], F32, name="s_col")
+            nc.sync.dma_start(out=s_col[:], in_=hh_scale.rearrange("o (g p t) -> p (o g) t", p=P, t=PACK))
             load_hh(0)
-            wz_raw = [load_weight(wz[0:512, :], "wz_raw0"), load_weight(wz[512:1024, :], "wz_raw1")]
+            wz_raw = [load_weight(wz[k * K_PASS : (k + 1) * K_PASS, :], "wz_raw%d" % k) for k in range(2)]
             load_hh(1)
-            bz_raw = keep.tile([P, 4], BF16, name="bz_raw")
-            nc.sync.dma_start(out=bz_raw[:], in_=bz.rearrange("(p t) -> p t", t=4))
+            bz_raw = keep.tile([P, PACK], BF16, name="bz_raw")
+            nc.sync.dma_start(out=bz_raw[:], in_=bz.rearrange("(p t) -> p t", t=PACK))
             wh_raw = load_weight(wh, "wh_raw")
             load_h(0)
             wd_raw = load_weight(wd, "wd_raw")
             load_hh(2)
+            load_h(1)
+            load_hh(3)
             c_sb = keep.tile([P, TILES * H], BF16, name="c_sb", align_bytes=256)
-            for g in range(1, GROUPS):
+            nc.sync.dma_start(out=c_sb[:], in_=c_rows)
+            for g in range(2, GROUPS):
                 load_h(g)
                 if g + 2 < GROUPS:
                     load_hh(g + 2)
-                if g == 1:
-                    nc.sync.dma_start(out=c_sb[:], in_=c_v)
 
             s_bank = []
             for k in range(2):
                 bank = fixed.tile([P, BANK], F32, name="s_bank%d" % k)
-                for t in range(4):
-                    nc.tensor.transpose(bank[:, t:BANK:4], s_col[:, k, t : t + 1].to_broadcast([P, P]), ident[:])
+                for t in range(PACK):
+                    nc.tensor.transpose(bank[:, t:BANK:PACK], s_col[:, k, t : t + 1].to_broadcast([P, P]), ident[:])
                 s_bank.append(bank)
 
         def quantize_weight(src, name):
-            width = src.shape[1] // 4
+            width = src.shape[1] // PACK
             codes = keep.tile([P, width], U32, name=name + "_codes", align_bytes=64)
             scales = keep.tile([P, width], U8, name=name + "_scales", align_bytes=64)
             nc.vector.quantize_mx(out=codes[:].bitcast(FP8X4), scales=scales[:], in_=src[:])
             return codes, scales
 
         def mx(out, lhs, l0, rhs, r0, start=True, stop=True):
-            n = out.shape[1]
+            width = out.shape[1]
             nc.tensor.matmul_mx(
                 out=out,
                 lhsT=lhs[0][:, l0 : l0 + P].bitcast(FP8X4),
                 lhsT_scale=lhs[1][:, l0 : l0 + P],
-                rhs=rhs[0][:, r0 : r0 + n].bitcast(FP8X4),
-                rhs_scale=rhs[1][:, r0 : r0 + n],
+                rhs=rhs[0][:, r0 : r0 + width].bitcast(FP8X4),
+                rhs_scale=rhs[1][:, r0 : r0 + width],
                 start=start,
                 stop=stop,
             )
 
         def interleave_wz(copy, k):
-            t = keep.tile([P, 4 * Z], BF16, name="wz_il%d" % k, align_bytes=64)
+            t = keep.tile([P, PACK * Z], BF16, name="wz_packed%d" % k, align_bytes=64)
             copy(
-                out=t[:].rearrange("p (t m j) -> p t m j", t=4, j=4),
-                in_=wz_raw[k][:].rearrange("p j (m t) -> p t m j", t=4),
+                out=t[:].rearrange("p (s m t) -> p s m t", s=PACK, t=PACK),
+                in_=wz_raw[k][:].rearrange("p t (m s) -> p s m t", s=PACK),
             )
             return t
 
-        def interleave(copy, raw, name):
-            t = keep.tile([P, 4 * raw.shape[2]], BF16, name=name, align_bytes=64)
-            copy(out=t[:].rearrange("p (n j) -> p n j", j=4), in_=raw[:].rearrange("p j n -> p n j"))
+        def interleave(raw, name):
+            t = keep.tile([P, PACK * raw.shape[2]], BF16, name=name, align_bytes=64)
+            nc.scalar.copy(out=t[:].rearrange("p (n t) -> p n t", t=PACK), in_=raw[:].rearrange("p t n -> p n t"))
             return t
 
-        scaled, staged, act_q, z_pairs = {}, {}, {}, {}
-        d_bank, beta_bank, r_sb, mod, pre, gates, ig, fc, c1, th = {}, {}, {}, {}, {}, {}, {}, {}, {}, {}
         weights = {}
-        halves = [(g, a, k) for g in range(GROUPS) for a in range(SIZES[g]) for k in range(2)]
+        scaled, staged, quantised, z_pairs = {}, {}, {}, {}
+        d_bank, beta_bank, r_sb, modulated, pre, gates, kept, gained, c1, tanh_c1 = ({} for i in range(10))
 
-        def cell_engine(g):
-            return nc.vector if g >= CELL_V else nc.gpsimd
-
-        def scale_hh(j):
-            if j >= len(halves):
-                return
-            g, a, k = halves[j]
+        def scale_hh(g, a, k):
             if k == 0:
                 scaled[(g, a)] = scaled_pool.tile([P, E], BF16, name="scaled", align_bytes=64)
             nc.vector.tensor_tensor(
-                out=scaled[(g, a)][:, k * BANK : (k + 1) * BANK],
-                in0=hh_raw[g][:, a * E + k * BANK : a * E + (k + 1) * BANK].bitcast(FP8),
+                out=scaled[(g, a)][:, k * K_PASS : (k + 1) * K_PASS],
+                in0=hh_raw[g][:, a * E + k * K_PASS : a * E + (k + 1) * K_PASS].bitcast(FP8),
                 in1=s_bank[k][:],
                 op=ALU.mult,
             )
 
         def staging(s, at_col, width):
             if s not in staged:
-                staged[s] = work.tile([P, 4 * STAGE_COLS], BF16, name="staged", align_bytes=64)
-            return staged[s][:, 4 * at_col : 4 * (at_col + width)]
+                staged[s] = work.tile([P, PACK * STEP_COLS], BF16, name="staged", align_bytes=64)
+            return staged[s][:, PACK * at_col : PACK * (at_col + width)]
 
-        def turn_hh(g):
-            nt = SIZES[g]
-            words = staging(g, HH_AT, 2 * nt * P).bitcast(F32).rearrange("p (k a n u) -> p k a n u", k=2, a=nt, u=2)
-            for a in range(nt):
-                src = scaled[(g, a)][:].bitcast(F32)
-                bank = ring.tile([P, BANK], F32, name="bank")
-                for k in range(2):
-                    for u in range(2):
-                        j = 2 * k + u
-                        nc.tensor.transpose(
-                            bank[:, j * P : (j + 1) * P], src[:, k * 256 + u : (k + 1) * 256 : 2], ident[:]
-                        )
-                nc.scalar.copy(out=words[:, :, a], in_=bank[:].rearrange("p (k u n) -> p k n u", u=2, k=2))
-
-        def quantize_step(s):
-            parts = [(at_col, per_tile * SIZES[g])
-                     for at_col, per_tile, g in ((Z_AT, P, s - 2), (HH_AT, 2 * P, s), (H_AT, P, s - 1))
-                     if 0 <= g < GROUPS]
-            if sum(w for at_col, w in parts) == STAGE_COLS:
-                parts = [(0, STAGE_COLS)]
-            codes = work.tile([P, STAGE_COLS], U32, name="act_codes", align_bytes=64)
-            scales = work.tile([P, STAGE_COLS], U8, name="act_scales", align_bytes=64)
-            for at_col, w in parts:
-                nc.vector.quantize_mx(
-                    out=codes[:, at_col : at_col + w].bitcast(FP8X4),
-                    scales=scales[:, at_col : at_col + w],
-                    in_=staging(s, at_col, w),
-                )
-            act_q[s] = (codes, scales)
-
-        def embed(g):
-            n = SIZES[g] * P
-            zp = work.tile([P, 2, n, 2], BF16, name="z_pairs", align_bytes=64)
+        def transpose_pass(bank, slot, pairs):
             for u in range(2):
-                bank = ring.tile([P, BANK], F32, name="bank")
-                for e in range(2):
-                    for k in range(2):
-                        mx(bank[:, e * n : (e + 1) * n], weights["wz", k], (2 * u + e) * P,
-                           act_q[g], HH_AT + k * n, k == 0, k == 1)
-                for e in range(2):
-                    t = 2 * u + e
-                    nc.scalar.activation(
-                        out=zp[:, u, :, e], in_=bank[:, e * n : (e + 1) * n], func=ACT.Identity,
-                        bias=weights["bz"][:, t : t + 1],
-                    )
-            z_pairs[g] = zp
+                nc.tensor.transpose(bank[:, (slot + u) * P : (slot + u + 1) * P], pairs[:, u:PAIRS:2], ident[:])
+
+        def turn_hh(g, a):
+            src = scaled[(g, a)][:].bitcast(F32)
+            bank = ring.tile([P, BANK], F32, name="bank")
+            for k in range(2):
+                transpose_pass(bank, 2 * k, src[:, k * PAIRS : (k + 1) * PAIRS])
+            dst = staging(g, HH_AT, 2 * N).bitcast(F32).rearrange("p (k a n u) -> p k a n u", k=2, a=PAIR, u=2)
+            nc.scalar.copy(out=dst[:, :, a], in_=bank[:].rearrange("p (k u n) -> p k n u", k=2, u=2))
 
         def turn_h(g):
-            nt = SIZES[g]
             src = h_raw[g][:].bitcast(F32)
             bank = ring.tile([P, BANK], F32, name="bank")
-            for a in range(nt):
-                for u in range(2):
-                    j = 2 * a + u
-                    nc.tensor.transpose(
-                        bank[:, j * P : (j + 1) * P], src[:, a * 256 + u : (a + 1) * 256 : 2], ident[:]
-                    )
-            (nc.vector.tensor_copy if g >= H_V else nc.scalar.copy)(
-                out=staging(g + 1, H_AT, nt * P).bitcast(F32).rearrange("p (a n u) -> p a n u", a=nt, u=2),
-                in_=bank[:, 0 : 2 * nt * P].rearrange("p (a u n) -> p a n u", a=nt, u=2),
+            for a in range(PAIR):
+                transpose_pass(bank, 2 * a, src[:, a * PAIRS : (a + 1) * PAIRS])
+            nc.scalar.copy(
+                out=staging(g + 1, H_AT, N).bitcast(F32).rearrange("p (a n u) -> p a n u", a=PAIR, u=2),
+                in_=bank[:].rearrange("p (a u n) -> p a n u", a=PAIR, u=2),
             )
 
+        def quantize_step(s):
+            parts = [
+                (at_col, width)
+                for at_col, width, g in ((Z_AT, N, s - 2), (HH_AT, 2 * N, s), (H_AT, N, s - 1))
+                if 0 <= g < GROUPS
+            ]
+            if len(parts) == 3:
+                parts = [(0, STEP_COLS)]
+            codes = work.tile([P, STEP_COLS], U32, name="step_codes", align_bytes=64)
+            scales = work.tile([P, STEP_COLS], U8, name="step_scales", align_bytes=64)
+            for at_col, width in parts:
+                nc.vector.quantize_mx(
+                    out=codes[:, at_col : at_col + width].bitcast(FP8X4),
+                    scales=scales[:, at_col : at_col + width],
+                    in_=staging(s, at_col, width),
+                )
+            quantised[s] = (codes, scales)
+
+        def embed(g, u):
+            if u == 0:
+                z_pairs[g] = keep.tile([P, 2, N, 2], BF16, name="shared%d" % (g % 2), align_bytes=64)
+            bank = ring.tile([P, BANK], F32, name="bank")
+            for e in range(2):
+                for k in range(2):
+                    mx(bank[:, e * N : (e + 1) * N], weights["wz", k], (2 * u + e) * P,
+                       quantised[g], HH_AT + k * N, start=k == 0, stop=k == 1)
+            for e in range(2):
+                t = 2 * u + e
+                nc.scalar.activation(
+                    out=z_pairs[g][:, u, :, e],
+                    in_=bank[:, e * N : (e + 1) * N],
+                    func=ACT.Identity,
+                    bias=weights["bz"][:, t : t + 1],
+                )
+
         def interleave_z(g):
+            pairs = z_pairs[g][:].rearrange("p u n e -> p (u n e)").bitcast(F32)
             nc.vector.tensor_copy(
-                out=staging(g + 2, Z_AT, SIZES[g] * P).bitcast(F32).rearrange("p (n u) -> p n u", u=2),
-                in_=z_pairs[g][:].rearrange("p u n e -> p (u n e)").bitcast(F32).rearrange("p (u n) -> p n u", u=2),
+                out=staging(g + 2, Z_AT, N).bitcast(F32).rearrange("p (n u) -> p n u", u=2),
+                in_=pairs.rearrange("p (u n) -> p n u", u=2),
             )
 
         def recur(g):
-            nt = SIZES[g]
             bank = ring.tile([P, BANK], F32, name="bank")
-            for a in range(nt):
-                mx(bank[:, a * G4 : (a + 1) * G4], act_q[g + 1], H_AT + a * P, weights["wh"], 0)
-            r = deep.tile([P, nt * G4], F32, name="r_sb")
-            (nc.vector.tensor_copy if g >= R_V else nc.scalar.copy)(out=r[:], in_=bank[:, 0 : nt * G4])
-            r_sb[g] = r
+            for a in range(PAIR):
+                mx(bank[:, a * G4 : (a + 1) * G4], quantised[g + 1], H_AT + a * P, weights["wh"], 0)
+            r_sb[g] = deep.tile([P, BANK], F32, name="r_sb")
+            nc.scalar.copy(out=r_sb[g][:], in_=bank[:])
 
         def generate(g):
-            d = fixed.tile([P, BANK], F32, name="d_bank")
-            beta = fixed.tile([P, BANK], F32, name="beta_bank")
-            for a in range(SIZES[g]):
-                mx(d[:, a * G4 : (a + 1) * G4], act_q[g + 2], Z_AT + a * P, weights["wd"], 0)
-                mx(beta[:, a * G4 : (a + 1) * G4], act_q[g + 2], Z_AT + a * P, weights["wd"], G4)
-            d_bank[g], beta_bank[g] = d, beta
+            d_bank[g] = fixed.tile([P, BANK], F32, name="d_bank")
+            beta_bank[g] = fixed.tile([P, BANK], F32, name="beta_bank")
+            for a in range(PAIR):
+                mx(d_bank[g][:, a * G4 : (a + 1) * G4], quantised[g + 2], Z_AT + a * P, weights["wd"], 0)
+                mx(beta_bank[g][:, a * G4 : (a + 1) * G4], quantised[g + 2], Z_AT + a * P, weights["wd"], G4)
 
         def modulate(g):
-            w = SIZES[g] * G4
-            t = work.tile([P, w], F32, name="mod")
+            modulated[g] = work.tile([P, BANK], F32, name="modulated")
             nc.vector.scalar_tensor_tensor(
-                out=t[:], in0=d_bank[g][:, 0:w], scalar=1.0, in1=r_sb[g][:], op0=ALU.add, op1=ALU.mult
+                out=modulated[g][:], in0=d_bank[g][:], scalar=1.0, in1=r_sb[g][:], op0=ALU.add, op1=ALU.mult
             )
-            mod[g] = t
 
         def add_beta(g):
-            w = SIZES[g] * G4
-            t = work.tile([P, w], F32, name="pre")
-            nc.vector.tensor_tensor(out=t[:], in0=beta_bank[g][:, 0:w], in1=mod[g][:], op=ALU.add)
-            pre[g] = t
+            pre[g] = work.tile([P, BANK], F32, name="pre")
+            nc.vector.tensor_tensor(out=pre[g][:], in0=beta_bank[g][:], in1=modulated[g][:], op=ALU.add)
 
         def activate(g):
-            t = work.tile([P, SIZES[g], 4, H], F32, name="gates")
             src = pre[g][:].rearrange("p (a q d) -> p a q d", q=4, d=H)
-            nc.scalar.activation(out=t[:, :, 2, :], in_=src[:, :, 2, :], func=ACT.Sigmoid, bias=1.0)
-            nc.scalar.activation(out=t[:, :, 1, :], in_=src[:, :, 1, :], func=ACT.Tanh)
-            nc.scalar.activation(out=t[:, :, 0:4:3, :], in_=src[:, :, 0:4:3, :], func=ACT.Sigmoid)
-            gates[g] = t
+            forget = work.tile([P, PAIR, H], F32, name="gate_forget")
+            nc.scalar.activation(out=forget[:], in_=src[:, :, 2, :], func=ACT.Sigmoid, bias=1.0)
+            candidate = work.tile([P, PAIR, H], F32, name="gate_candidate")
+            nc.scalar.activation(out=candidate[:], in_=src[:, :, 1, :], func=ACT.Tanh)
+            in_out = work.tile([P, PAIR, 2, H], F32, name="gate_in_out")
+            nc.scalar.activation(out=in_out[:], in_=src[:, :, 0:4:3, :], func=ACT.Sigmoid)
+            gates[g] = (forget, candidate, in_out)
 
-        def products(g):
-            f = work.tile([P, SIZES[g], H], F32, name="fc")
+        def products(g, engine):
+            forget, candidate, in_out = gates[g]
+            kept[g] = keep.tile([P, PAIR, H], F32, name="shared%d" % ((g + 3) % 2), align_bytes=64)
             c_g = c_sb[:, cols(g, H)].rearrange("p (a d) -> p a d", d=H)
-            cell_engine(g).tensor_tensor(out=f[:], in0=gates[g][:, :, 2, :], in1=c_g, op=ALU.mult)
-            fc[g] = f
-            t = work.tile([P, SIZES[g], H], F32, name="ig")
-            cell_engine(g).tensor_tensor(out=t[:], in0=gates[g][:, :, 0, :], in1=gates[g][:, :, 1, :], op=ALU.mult)
-            ig[g] = t
+            engine.tensor_tensor(out=kept[g][:], in0=forget[:], in1=c_g, op=ALU.mult)
+            gained[g] = work.tile([P, PAIR, H], F32, name="gained")
+            engine.tensor_tensor(out=gained[g][:], in0=in_out[:, :, 0, :], in1=candidate[:], op=ALU.mult)
 
-        def new_cell(g):
-            t = deep.tile([P, SIZES[g], H], F32, name="c1")
-            cell_engine(g).tensor_tensor(out=t[:], in0=fc[g][:], in1=ig[g][:], op=ALU.add)
-            nc.sync.dma_start(out=c1_v[:, cols(g, H)], in_=t[:].rearrange("p a d -> p (a d)"))
-            c1[g] = t
+        def new_cell(g, engine):
+            c1[g] = deep.tile([P, PAIR, H], F32, name="c1")
+            engine.tensor_tensor(out=c1[g][:], in0=kept[g][:], in1=gained[g][:], op=ALU.add)
+            nc.sync.dma_start(out=c1_rows[:, cols(g, H)], in_=c1[g][:].rearrange("p a d -> p (a d)"))
 
         def squash(g):
-            t = work.tile([P, SIZES[g], H], F32, name="th")
-            nc.scalar.activation(out=t[:], in_=c1[g][:], func=ACT.Tanh)
-            th[g] = t
+            tanh_c1[g] = work.tile([P, PAIR, H], F32, name="tanh_c1")
+            nc.scalar.activation(out=tanh_c1[g][:], in_=c1[g][:], func=ACT.Tanh)
 
-        def new_state(g):
-            t = deep.tile([P, SIZES[g], H], F32, name="h1")
-            cell_engine(g).tensor_tensor(out=t[:], in0=gates[g][:, :, 3, :], in1=th[g][:], op=ALU.mult)
-            nc.sync.dma_start(out=h1_v[:, cols(g, H)], in_=t[:].rearrange("p a d -> p (a d)"))
+        def new_state(g, engine):
+            h1 = deep.tile([P, PAIR, H], F32, name="h1")
+            engine.tensor_tensor(out=h1[:], in0=gates[g][2][:, :, 1, :], in1=tanh_c1[g][:], op=ALU.mult)
+            nc.sync.dma_start(out=h1_rows[:, cols(g, H)], in_=h1[:].rearrange("p a d -> p (a d)"))
 
-        def at(fn, g):
+        def at(stage, g, *args):
             if 0 <= g < GROUPS:
-                fn(g)
+                stage(g, *args)
 
         def step(s):
-            j = 2 * AHEAD + 4 * s
-            at(turn_hh, s)
-            if s == 0:
-                weights["wh_il"] = interleave(nc.scalar.copy, wh_raw, "wh_il")
-                weights["wd_il"] = interleave(nc.scalar.copy, wd_raw, "wd_il")
-            scale_hh(j)
-            at(add_beta, s - 3)
+            cell_engine = nc.gpsimd if s < SCALING_STEPS else nc.vector
+            at(add_beta, s - 4)
+            at(turn_hh, s, 0)
+            at(embed, s - 1, 0)
+            at(turn_hh, s, 1)
+            at(embed, s - 1, 1)
+            at(scale_hh, s + 1, 0, 0)
+            at(scale_hh, s + 1, 0, 1)
+            at(scale_hh, s + 1, 1, 0)
             if s < GROUPS + 2:
                 quantize_step(s)
             if s == 1:
-                weights["wh"] = quantize_weight(weights["wh_il"], "wh")
-                weights["wd"] = quantize_weight(weights["wd_il"], "wd")
-            at(embed, s - 1)
+                weights["wh"] = quantize_weight(weights["wh_packed"], "wh")
+                weights["wd"] = quantize_weight(weights["wd_packed"], "wd")
             at(interleave_z, s - 1)
-            at(squash, s - 4)
-            at(activate, s - 3)
-            at(new_state, s - 4)
-            at(products, s - 3)
-            at(new_cell, s - 3)
-            scale_hh(j + 1)
-            scale_hh(j + 2)
-            scale_hh(j + 3)
             at(turn_h, s)
-            at(generate, s - 2)
-            at(recur, s - 1)
-            at(modulate, s - 2)
+            at(activate, s - 4)
+            at(squash, s - LAST_LAG)
+            at(products, s - 4, cell_engine)
+            at(new_state, s - LAST_LAG, cell_engine)
+            at(new_cell, s - 4, cell_engine)
+            at(recur, s - 2)
+            at(generate, s - 3)
+            at(modulate, s - 3)
+            at(scale_hh, s + 1, 1, 1)
 
         with tc.manual_schedule():
-            wz_il0 = interleave_wz(nc.scalar.copy, 0)
-            for j in range(4):
-                scale_hh(j)
-            wz_il1 = interleave_wz(nc.vector.tensor_copy, 1)
-            weights["wz", 0] = quantize_weight(wz_il0, "wz0")
-            bz_f = keep.tile([P, 4], F32, name="bz_f")
-            nc.vector.tensor_copy(out=bz_f[:], in_=bz_raw[:])
-            weights["bz"] = bz_f
-            weights["wz", 1] = quantize_weight(wz_il1, "wz1")
-            for j in range(4, 2 * AHEAD):
-                scale_hh(j)
-
-            for s in range(PINNED):
+            wz_packed0 = interleave_wz(nc.scalar.copy, 0)
+            for k in range(2):
+                for a in range(PAIR):
+                    scale_hh(0, a, k)
+            wz_packed1 = interleave_wz(nc.vector.tensor_copy, 1)
+            for a in range(PAIR):
+                turn_hh(0, a)
+            weights["wz", 0] = quantize_weight(wz_packed0, "wz0")
+            weights["bz"] = keep.tile([P, PACK], F32, name="bz_f32")
+            nc.vector.tensor_copy(out=weights["bz"][:], in_=bz_raw[:])
+            quantize_step(0)
+            weights["wz", 1] = quantize_weight(wz_packed1, "wz1")
+            weights["wh_packed"] = interleave(wh_raw, "wh_packed")
+            weights["wd_packed"] = interleave(wd_raw, "wd_packed")
+            turn_h(0)
+            for a in range(PAIR):
+                for k in range(2):
+                    scale_hh(1, a, k)
+            for s in range(1, SCALING_STEPS):
                 step(s)
-        for s in range(PINNED, GROUPS + 4):
+
+        for s in range(SCALING_STEPS, GROUPS + LAST_LAG):
             step(s)

@@ -28,7 +28,8 @@ GROUPS = TILES // PAIR
 
 HH_AT, H_AT, Z_AT, STEP_COLS = 0, 2 * N, 3 * N, 4 * N
 
-SCALING_STEPS = GROUPS - 1
+PINNED_STEPS = GROUPS - 1
+GPSIMD_GROUPS = GROUPS - 6
 LAST_LAG = 5
 
 
@@ -75,6 +76,11 @@ def tile_hyperlstmgeneratedscalebiasstep_t_kernel(
             ident = keep.tile([P, P], F32, name="ident")
             make_identity(nc, ident[:])
 
+            warm_in = keep.tile([P, 1], F32, name="warm_in")
+            nc.vector.memset(warm_in[:], 0.0)
+            warm_out = keep.tile([P, 1], F32, name="warm_out")
+            nc.scalar.activation(out=warm_out[:], in_=warm_in[:], func=ACT.Sigmoid)
+
             s_col = keep.tile([P, 2, PACK], F32, name="s_col")
             nc.sync.dma_start(out=s_col[:], in_=hh_scale.rearrange("o (g p t) -> p (o g) t", p=P, t=PACK))
             load_hh(0)
@@ -86,9 +92,9 @@ def tile_hyperlstmgeneratedscalebiasstep_t_kernel(
             load_h(0)
             wd_raw = load_weight(wd, "wd_raw")
             load_hh(2)
+            c_sb = keep.tile([P, TILES * H], BF16, name="c_sb", align_bytes=256)
             load_h(1)
             load_hh(3)
-            c_sb = keep.tile([P, TILES * H], BF16, name="c_sb", align_bytes=256)
             nc.sync.dma_start(out=c_sb[:], in_=c_rows)
             for g in range(2, GROUPS):
                 load_h(g)
@@ -158,11 +164,11 @@ def tile_hyperlstmgeneratedscalebiasstep_t_kernel(
                 nc.tensor.transpose(bank[:, (slot + u) * P : (slot + u + 1) * P], pairs[:, u:PAIRS:2], ident[:])
 
         def turn_hh(g, a):
+            dst = staging(g, HH_AT, 2 * N).bitcast(F32).rearrange("p (k a n u) -> p k a n u", k=2, a=PAIR, u=2)
             src = scaled[(g, a)][:].bitcast(F32)
             bank = ring.tile([P, BANK], F32, name="bank")
             for k in range(2):
                 transpose_pass(bank, 2 * k, src[:, k * PAIRS : (k + 1) * PAIRS])
-            dst = staging(g, HH_AT, 2 * N).bitcast(F32).rearrange("p (k a n u) -> p k a n u", k=2, a=PAIR, u=2)
             nc.scalar.copy(out=dst[:, :, a], in_=bank[:].rearrange("p (k u n) -> p k n u", k=2, u=2))
 
         def turn_h(g):
@@ -195,7 +201,7 @@ def tile_hyperlstmgeneratedscalebiasstep_t_kernel(
 
         def embed(g, u):
             if u == 0:
-                z_pairs[g] = keep.tile([P, 2, N, 2], BF16, name="shared%d" % (g % 2), align_bytes=64)
+                z_pairs[g] = work.tile([P, 2, N, 2], BF16, name="z_pairs", align_bytes=64)
             bank = ring.tile([P, BANK], F32, name="bank")
             for e in range(2):
                 for k in range(2):
@@ -251,26 +257,29 @@ def tile_hyperlstmgeneratedscalebiasstep_t_kernel(
             nc.scalar.activation(out=in_out[:], in_=src[:, :, 0:4:3, :], func=ACT.Sigmoid)
             gates[g] = (forget, candidate, in_out)
 
-        def products(g, engine):
-            forget, candidate, in_out = gates[g]
-            kept[g] = keep.tile([P, PAIR, H], F32, name="shared%d" % ((g + 3) % 2), align_bytes=64)
-            c_g = c_sb[:, cols(g, H)].rearrange("p (a d) -> p a d", d=H)
-            engine.tensor_tensor(out=kept[g][:], in0=forget[:], in1=c_g, op=ALU.mult)
-            gained[g] = work.tile([P, PAIR, H], F32, name="gained")
-            engine.tensor_tensor(out=gained[g][:], in0=in_out[:, :, 0, :], in1=candidate[:], op=ALU.mult)
+        def cell_engine(g):
+            return nc.gpsimd if g < GPSIMD_GROUPS else nc.vector
 
-        def new_cell(g, engine):
+        def products(g):
+            forget, candidate, in_out = gates[g]
+            kept[g] = work.tile([P, PAIR, H], F32, name="kept")
+            c_g = c_sb[:, cols(g, H)].rearrange("p (a d) -> p a d", d=H)
+            cell_engine(g).tensor_tensor(out=kept[g][:], in0=forget[:], in1=c_g, op=ALU.mult)
+            gained[g] = work.tile([P, PAIR, H], F32, name="gained")
+            cell_engine(g).tensor_tensor(out=gained[g][:], in0=in_out[:, :, 0, :], in1=candidate[:], op=ALU.mult)
+
+        def new_cell(g):
             c1[g] = deep.tile([P, PAIR, H], F32, name="c1")
-            engine.tensor_tensor(out=c1[g][:], in0=kept[g][:], in1=gained[g][:], op=ALU.add)
+            cell_engine(g).tensor_tensor(out=c1[g][:], in0=kept[g][:], in1=gained[g][:], op=ALU.add)
             nc.sync.dma_start(out=c1_rows[:, cols(g, H)], in_=c1[g][:].rearrange("p a d -> p (a d)"))
 
         def squash(g):
             tanh_c1[g] = work.tile([P, PAIR, H], F32, name="tanh_c1")
             nc.scalar.activation(out=tanh_c1[g][:], in_=c1[g][:], func=ACT.Tanh)
 
-        def new_state(g, engine):
+        def new_state(g):
             h1 = deep.tile([P, PAIR, H], F32, name="h1")
-            engine.tensor_tensor(out=h1[:], in0=gates[g][2][:, :, 1, :], in1=tanh_c1[g][:], op=ALU.mult)
+            cell_engine(g).tensor_tensor(out=h1[:], in0=gates[g][2][:, :, 1, :], in1=tanh_c1[g][:], op=ALU.mult)
             nc.sync.dma_start(out=h1_rows[:, cols(g, H)], in_=h1[:].rearrange("p a d -> p (a d)"))
 
         def at(stage, g, *args):
@@ -278,15 +287,14 @@ def tile_hyperlstmgeneratedscalebiasstep_t_kernel(
                 stage(g, *args)
 
         def step(s):
-            cell_engine = nc.gpsimd if s < SCALING_STEPS else nc.vector
             at(add_beta, s - 4)
             at(turn_hh, s, 0)
             at(embed, s - 1, 0)
             at(turn_hh, s, 1)
             at(embed, s - 1, 1)
-            at(scale_hh, s + 1, 0, 0)
-            at(scale_hh, s + 1, 0, 1)
             at(scale_hh, s + 1, 1, 0)
+            at(scale_hh, s + 1, 1, 1)
+            at(scale_hh, s + 2, 0, 0)
             if s < GROUPS + 2:
                 quantize_step(s)
             if s == 1:
@@ -296,13 +304,13 @@ def tile_hyperlstmgeneratedscalebiasstep_t_kernel(
             at(turn_h, s)
             at(activate, s - 4)
             at(squash, s - LAST_LAG)
-            at(products, s - 4, cell_engine)
-            at(new_state, s - LAST_LAG, cell_engine)
-            at(new_cell, s - 4, cell_engine)
+            at(products, s - 4)
+            at(new_state, s - LAST_LAG)
+            at(new_cell, s - 4)
             at(recur, s - 2)
             at(generate, s - 3)
             at(modulate, s - 3)
-            at(scale_hh, s + 1, 1, 1)
+            at(scale_hh, s + 2, 0, 1)
 
         with tc.manual_schedule():
             wz_packed0 = interleave_wz(nc.scalar.copy, 0)
@@ -320,11 +328,11 @@ def tile_hyperlstmgeneratedscalebiasstep_t_kernel(
             weights["wh_packed"] = interleave(wh_raw, "wh_packed")
             weights["wd_packed"] = interleave(wd_raw, "wd_packed")
             turn_h(0)
-            for a in range(PAIR):
+            for g, a in ((1, 0), (1, 1), (2, 0)):
                 for k in range(2):
-                    scale_hh(1, a, k)
-            for s in range(1, SCALING_STEPS):
+                    scale_hh(g, a, k)
+            for s in range(1, PINNED_STEPS):
                 step(s)
 
-        for s in range(SCALING_STEPS, GROUPS + LAST_LAG):
+        for s in range(PINNED_STEPS, GROUPS + LAST_LAG):
             step(s)

from contextlib import ExitStack

import concourse.mybir as mybir
from concourse.masks import make_identity

B, E, Z, R, H = 4096, 1024, 512, 512, 64
G4 = 4 * H
FLOPS = 2 * B * (E * Z + Z * 2 * G4 + R * G4)

F32 = mybir.dt.float32
BF16 = mybir.dt.bfloat16
U32 = mybir.dt.uint32
U8 = mybir.dt.uint8
FP8 = mybir.dt.float8_e4m3fn
FP8X4 = mybir.dt.float8_e4m3fn_x4
ACT = mybir.ActivationFunctionType
ALU = mybir.AluOpType

P = 128
PACK = 4
K_PASS = P * PACK
PAIRS = K_PASS // 2
BANK = 512
TILES = B // P
PAIR = 2
N = PAIR * P
GROUPS = TILES // PAIR

HH_AT, H_AT, Z_AT, STEP_COLS = 0, 2 * N, 3 * N, 4 * N

PINNED_STEPS = GROUPS - 1
GPSIMD_GROUPS = GROUPS - 6
LAST_LAG = 5


def tile_hyperlstmgeneratedscalebiasstep_t_kernel(
    tc, hh_bytes, hh_scale, h, c, wz, bz, wd, wh, out_0, out_1
):
    nc = tc.nc
    hh_rows = hh_bytes.rearrange("(p j) k -> p (j k)", j=TILES)
    h_rows = h.rearrange("(p j) k -> p (j k)", j=TILES)
    c_rows = c.rearrange("(p j) d -> p (j d)", j=TILES)
    h1_rows = out_0.rearrange("(p j) d -> p (j d)", j=TILES)
    c1_rows = out_1.rearrange("(p j) d -> p (j d)", j=TILES)

    def cols(g, width):
        return slice(g * PAIR * width, (g + 1) * PAIR * width)

    with ExitStack() as ctx:
        keep = ctx.enter_context(tc.tile_pool(name="keep", bufs=1))
        inputs = ctx.enter_context(tc.tile_pool(name="inputs", bufs=GROUPS))
        work = ctx.enter_context(tc.tile_pool(name="work", bufs=3))
        deep = ctx.enter_context(tc.tile_pool(name="deep", bufs=4))
        scaled_pool = ctx.enter_context(tc.tile_pool(name="scaled", bufs=6))
        ring = ctx.enter_context(tc.psum_pool(name="ring", bufs=4))
        fixed = ctx.enter_context(tc.psum_pool(name="fixed", bufs=1))

        hh_raw, h_raw = {}, {}

        def load_hh(g):
            t = inputs.tile([P, PAIR * E], U8, name="hh_codes", align_bytes=256)
            nc.sync.dma_start(out=t[:], in_=hh_rows[:, cols(g, E)])
            hh_raw[g] = t

        def load_h(g):
            t = inputs.tile([P, PAIR * R], BF16, name="h_values", align_bytes=256)
            nc.sync.dma_start(out=t[:], in_=h_rows[:, cols(g, R)])
            h_raw[g] = t

        def load_weight(rows, name):
            t = keep.tile([P, PACK, rows.shape[1]], BF16, name=name, align_bytes=256)
            nc.sync.dma_start(out=t[:], in_=rows.rearrange("(p t) n -> p t n", t=PACK))
            return t

        with tc.manual_schedule():
            ident = keep.tile([P, P], F32, name="ident")
            make_identity(nc, ident[:])

            warm_in = keep.tile([P, 1], F32, name="warm_in")
            nc.vector.memset(warm_in[:], 0.0)
            warm_out = keep.tile([P, 1], F32, name="warm_out")
            nc.scalar.activation(out=warm_out[:], in_=warm_in[:], func=ACT.Sigmoid)

            s_col = keep.tile([P, 2, PACK], F32, name="s_col")
            nc.sync.dma_start(out=s_col[:], in_=hh_scale.rearrange("o (g p t) -> p (o g) t", p=P, t=PACK))
            load_hh(0)
            wz_raw = [load_weight(wz[k * K_PASS : (k + 1) * K_PASS, :], "wz_raw%d" % k) for k in range(2)]
            load_hh(1)
            bz_raw = keep.tile([P, PACK], BF16, name="bz_raw")
            nc.sync.dma_start(out=bz_raw[:], in_=bz.rearrange("(p t) -> p t", t=PACK))
            wh_raw = load_weight(wh, "wh_raw")
            load_h(0)
            wd_raw = load_weight(wd, "wd_raw")
            load_hh(2)
            c_sb = keep.tile([P, TILES * H], BF16, name="c_sb", align_bytes=256)
            load_h(1)
            load_hh(3)
            nc.sync.dma_start(out=c_sb[:], in_=c_rows)
            for g in range(2, GROUPS):
                load_h(g)
                if g + 2 < GROUPS:
                    load_hh(g + 2)

            s_bank = []
            for k in range(2):
                bank = fixed.tile([P, BANK], F32, name="s_bank%d" % k)
                for t in range(PACK):
                    nc.tensor.transpose(bank[:, t:BANK:PACK], s_col[:, k, t : t + 1].to_broadcast([P, P]), ident[:])
                s_bank.append(bank)

        def quantize_weight(src, name):
            width = src.shape[1] // PACK
            codes = keep.tile([P, width], U32, name=name + "_codes", align_bytes=64)
            scales = keep.tile([P, width], U8, name=name + "_scales", align_bytes=64)
            nc.vector.quantize_mx(out=codes[:].bitcast(FP8X4), scales=scales[:], in_=src[:])
            return codes, scales

        def mx(out, lhs, l0, rhs, r0, start=True, stop=True):
            width = out.shape[1]
            nc.tensor.matmul_mx(
                out=out,
                lhsT=lhs[0][:, l0 : l0 + P].bitcast(FP8X4),
                lhsT_scale=lhs[1][:, l0 : l0 + P],
                rhs=rhs[0][:, r0 : r0 + width].bitcast(FP8X4),
                rhs_scale=rhs[1][:, r0 : r0 + width],
                start=start,
                stop=stop,
            )

        def interleave_wz(copy, k):
            t = keep.tile([P, PACK * Z], BF16, name="wz_packed%d" % k, align_bytes=64)
            copy(
                out=t[:].rearrange("p (s m t) -> p s m t", s=PACK, t=PACK),
                in_=wz_raw[k][:].rearrange("p t (m s) -> p s m t", s=PACK),
            )
            return t

        def interleave(raw, name):
            t = keep.tile([P, PACK * raw.shape[2]], BF16, name=name, align_bytes=64)
            nc.scalar.copy(out=t[:].rearrange("p (n t) -> p n t", t=PACK), in_=raw[:].rearrange("p t n -> p n t"))
            return t

        weights = {}
        scaled, staged, quantised, z_pairs = {}, {}, {}, {}
        d_bank, beta_bank, r_sb, modulated, pre, gates, kept, gained, c1, tanh_c1 = ({} for i in range(10))

        def scale_hh(g, a, k):
            if k == 0:
                scaled[(g, a)] = scaled_pool.tile([P, E], BF16, name="scaled", align_bytes=64)
            nc.vector.tensor_tensor(
                out=scaled[(g, a)][:, k * K_PASS : (k + 1) * K_PASS],
                in0=hh_raw[g][:, a * E + k * K_PASS : a * E + (k + 1) * K_PASS].bitcast(FP8),
                in1=s_bank[k][:],
                op=ALU.mult,
            )

        def staging(s, at_col, width):
            if s not in staged:
                staged[s] = work.tile([P, PACK * STEP_COLS], BF16, name="staged", align_bytes=64)
            return staged[s][:, PACK * at_col : PACK * (at_col + width)]

        def transpose_pass(bank, slot, pairs):
            for u in range(2):
                nc.tensor.transpose(bank[:, (slot + u) * P : (slot + u + 1) * P], pairs[:, u:PAIRS:2], ident[:])

        def turn_hh(g, a):
            dst = staging(g, HH_AT, 2 * N).bitcast(F32).rearrange("p (k a n u) -> p k a n u", k=2, a=PAIR, u=2)
            src = scaled[(g, a)][:].bitcast(F32)
            bank = ring.tile([P, BANK], F32, name="bank")
            for k in range(2):
                transpose_pass(bank, 2 * k, src[:, k * PAIRS : (k + 1) * PAIRS])
            nc.scalar.copy(out=dst[:, :, a], in_=bank[:].rearrange("p (k u n) -> p k n u", k=2, u=2))

        def turn_h(g):
            src = h_raw[g][:].bitcast(F32)
            bank = ring.tile([P, BANK], F32, name="bank")
            for a in range(PAIR):
                transpose_pass(bank, 2 * a, src[:, a * PAIRS : (a + 1) * PAIRS])
            nc.scalar.copy(
                out=staging(g + 1, H_AT, N).bitcast(F32).rearrange("p (a n u) -> p a n u", a=PAIR, u=2),
                in_=bank[:].rearrange("p (a u n) -> p a n u", a=PAIR, u=2),
            )

        def quantize_step(s):
            parts = [
                (at_col, width)
                for at_col, width, g in ((Z_AT, N, s - 2), (HH_AT, 2 * N, s), (H_AT, N, s - 1))
                if 0 <= g < GROUPS
            ]
            if len(parts) == 3:
                parts = [(0, STEP_COLS)]
            codes = work.tile([P, STEP_COLS], U32, name="step_codes", align_bytes=64)
            scales = work.tile([P, STEP_COLS], U8, name="step_scales", align_bytes=64)
            for at_col, width in parts:
                nc.vector.quantize_mx(
                    out=codes[:, at_col : at_col + width].bitcast(FP8X4),
                    scales=scales[:, at_col : at_col + width],
                    in_=staging(s, at_col, width),
                )
            quantised[s] = (codes, scales)

        def embed(g, u):
            if u == 0:
                z_pairs[g] = work.tile([P, 2, N, 2], BF16, name="z_pairs", align_bytes=64)
            bank = ring.tile([P, BANK], F32, name="bank")
            for e in range(2):
                for k in range(2):
                    mx(bank[:, e * N : (e + 1) * N], weights["wz", k], (2 * u + e) * P,
                       quantised[g], HH_AT + k * N, start=k == 0, stop=k == 1)
            for e in range(2):
                t = 2 * u + e
                nc.scalar.activation(
                    out=z_pairs[g][:, u, :, e],
                    in_=bank[:, e * N : (e + 1) * N],
                    func=ACT.Identity,
                    bias=weights["bz"][:, t : t + 1],
                )

        def interleave_z(g):
            pairs = z_pairs[g][:].rearrange("p u n e -> p (u n e)").bitcast(F32)
            nc.vector.tensor_copy(
                out=staging(g + 2, Z_AT, N).bitcast(F32).rearrange("p (n u) -> p n u", u=2),
                in_=pairs.rearrange("p (u n) -> p n u", u=2),
            )

        def recur(g):
            bank = ring.tile([P, BANK], F32, name="bank")
            for a in range(PAIR):
                mx(bank[:, a * G4 : (a + 1) * G4], quantised[g + 1], H_AT + a * P, weights["wh"], 0)
            r_sb[g] = deep.tile([P, BANK], F32, name="r_sb")
            nc.scalar.copy(out=r_sb[g][:], in_=bank[:])

        def generate(g):
            d_bank[g] = fixed.tile([P, BANK], F32, name="d_bank")
            beta_bank[g] = fixed.tile([P, BANK], F32, name="beta_bank")
            for a in range(PAIR):
                mx(d_bank[g][:, a * G4 : (a + 1) * G4], quantised[g + 2], Z_AT + a * P, weights["wd"], 0)
                mx(beta_bank[g][:, a * G4 : (a + 1) * G4], quantised[g + 2], Z_AT + a * P, weights["wd"], G4)

        def modulate(g):
            modulated[g] = work.tile([P, BANK], F32, name="modulated")
            nc.vector.scalar_tensor_tensor(
                out=modulated[g][:], in0=d_bank[g][:], scalar=1.0, in1=r_sb[g][:], op0=ALU.add, op1=ALU.mult
            )

        def add_beta(g):
            pre[g] = work.tile([P, BANK], F32, name="pre")
            nc.vector.tensor_tensor(out=pre[g][:], in0=beta_bank[g][:], in1=modulated[g][:], op=ALU.add)

        def activate(g):
            src = pre[g][:].rearrange("p (a q d) -> p a q d", q=4, d=H)
            forget = work.tile([P, PAIR, H], F32, name="gate_forget")
            nc.scalar.activation(out=forget[:], in_=src[:, :, 2, :], func=ACT.Sigmoid, bias=1.0)
            candidate = work.tile([P, PAIR, H], F32, name="gate_candidate")
            nc.scalar.activation(out=candidate[:], in_=src[:, :, 1, :], func=ACT.Tanh)
            in_out = work.tile([P, PAIR, 2, H], F32, name="gate_in_out")
            nc.scalar.activation(out=in_out[:], in_=src[:, :, 0:4:3, :], func=ACT.Sigmoid)
            gates[g] = (forget, candidate, in_out)

        def cell_engine(g):
            return nc.gpsimd if g < GPSIMD_GROUPS else nc.vector

        def products(g):
            forget, candidate, in_out = gates[g]
            kept[g] = work.tile([P, PAIR, H], F32, name="kept")
            c_g = c_sb[:, cols(g, H)].rearrange("p (a d) -> p a d", d=H)
            cell_engine(g).tensor_tensor(out=kept[g][:], in0=forget[:], in1=c_g, op=ALU.mult)
            gained[g] = work.tile([P, PAIR, H], F32, name="gained")
            cell_engine(g).tensor_tensor(out=gained[g][:], in0=in_out[:, :, 0, :], in1=candidate[:], op=ALU.mult)

        def new_cell(g):
            c1[g] = deep.tile([P, PAIR, H], F32, name="c1")
            cell_engine(g).tensor_tensor(out=c1[g][:], in0=kept[g][:], in1=gained[g][:], op=ALU.add)
            nc.sync.dma_start(out=c1_rows[:, cols(g, H)], in_=c1[g][:].rearrange("p a d -> p (a d)"))

        def squash(g):
            tanh_c1[g] = work.tile([P, PAIR, H], F32, name="tanh_c1")
            nc.scalar.activation(out=tanh_c1[g][:], in_=c1[g][:], func=ACT.Tanh)

        def new_state(g):
            h1 = deep.tile([P, PAIR, H], F32, name="h1")
            cell_engine(g).tensor_tensor(out=h1[:], in0=gates[g][2][:, :, 1, :], in1=tanh_c1[g][:], op=ALU.mult)
            nc.sync.dma_start(out=h1_rows[:, cols(g, H)], in_=h1[:].rearrange("p a d -> p (a d)"))

        def at(stage, g, *args):
            if 0 <= g < GROUPS:
                stage(g, *args)

        def step(s):
            at(add_beta, s - 4)
            at(turn_hh, s, 0)
            at(embed, s - 1, 0)
            at(turn_hh, s, 1)
            at(embed, s - 1, 1)
            at(scale_hh, s + 1, 1, 0)
            at(scale_hh, s + 1, 1, 1)
            at(scale_hh, s + 2, 0, 0)
            if s < GROUPS + 2:
                quantize_step(s)
            if s == 1:
                weights["wh"] = quantize_weight(weights["wh_packed"], "wh")
                weights["wd"] = quantize_weight(weights["wd_packed"], "wd")
            at(interleave_z, s - 1)
            at(turn_h, s)
            at(activate, s - 4)
            at(squash, s - LAST_LAG)
            at(products, s - 4)
            at(new_state, s - LAST_LAG)
            at(new_cell, s - 4)
            at(recur, s - 2)
            at(generate, s - 3)
            at(modulate, s - 3)
            at(scale_hh, s + 2, 0, 1)

        with tc.manual_schedule():
            wz_packed0 = interleave_wz(nc.scalar.copy, 0)
            for k in range(2):
                for a in range(PAIR):
                    scale_hh(0, a, k)
            wz_packed1 = interleave_wz(nc.vector.tensor_copy, 1)
            for a in range(PAIR):
                turn_hh(0, a)
            weights["wz", 0] = quantize_weight(wz_packed0, "wz0")
            weights["bz"] = keep.tile([P, PACK], F32, name="bz_f32")
            nc.vector.tensor_copy(out=weights["bz"][:], in_=bz_raw[:])
            quantize_step(0)
            weights["wz", 1] = quantize_weight(wz_packed1, "wz1")
            weights["wh_packed"] = interleave(wh_raw, "wh_packed")
            weights["wd_packed"] = interleave(wd_raw, "wd_packed")
            turn_h(0)
            for g, a in ((1, 0), (1, 1), (2, 0)):
                for k in range(2):
                    scale_hh(g, a, k)
            for s in range(1, PINNED_STEPS):
                step(s)

        for s in range(PINNED_STEPS, GROUPS + LAST_LAG):
            step(s)
